import numpy as np
import ml_dtypes


def mxq(x, axis, fmt="e4m3"):
    dtype, down = {"e4m3": (ml_dtypes.float8_e4m3fn, 7), "e5m2": (ml_dtypes.float8_e5m2, 14)}[fmt]
    v = np.moveaxis(np.asarray(x, np.float32).astype(ml_dtypes.bfloat16).astype(np.float64), axis, -1)
    blocks = v.reshape(v.shape[:-1] + (-1, 32))
    amax = np.abs(blocks).max(-1, keepdims=True)
    byte = np.maximum(np.where(amax > 0, np.frexp(amax)[1] - 1 + 127, 0) - down, 1)
    scale = np.exp2(byte - 127.0)
    codes = (blocks / scale).astype(np.float32).astype(dtype).astype(np.float64)
    return np.moveaxis((codes * scale).reshape(v.shape), -1, axis)


WIDE = False


def mx_kscale(k):
    if not WIDE:
        return np.ones(k)
    levels = np.array([10, -10, 5, -5, 0])
    if k % 512:
        return np.exp2(np.random.permutation(np.resize(levels, k // 32))).repeat(32)
    a = np.empty((k // 512, 16))
    for p in range(k // 512):
        a[p, :8] = np.random.permutation(np.resize(levels, 8))
        for g in range(8):
            far = levels[np.abs(levels - a[p, g]) >= 10]
            a[p, g + 8] = far[np.random.randint(len(far))]
    return np.exp2(a.ravel()).repeat(32)


def f64(x):
    return np.asarray(x).astype(np.float64)


def striped(idx):
    return np.tile(idx.reshape(-1, 16).T, (8, 1)).astype(np.uint16)


def unstriped(offs):
    return offs[:16].T.reshape(-1).astype(np.int64)


def pack_weight(w):
    k, n = w.shape
    w = f64(np.asarray(w, np.float32).astype(ml_dtypes.bfloat16)).reshape(k // 32, 32, n)
    amax = np.abs(w).max(1)
    byte = np.clip(np.where(amax > 0, np.frexp(amax)[1] - 1 + 127 - 7, 1), 1, 254)
    scaled = (w * np.exp2(127.0 - byte)[:, None, :]).reshape(k, n).astype(np.float32)
    words = np.ascontiguousarray(scaled.reshape(k // 512, 128, 4, n).transpose(0, 1, 3, 2)).astype(ml_dtypes.float8_e4m3fn).view(np.uint8)
    return words, np.ascontiguousarray(byte.astype(np.uint8).reshape(k // 512, 16, n))


def unpack_weight(words, scales):
    g, p, n, _ = words.shape
    vals = np.ascontiguousarray(words).view(ml_dtypes.float8_e4m3fn).astype(np.float64) * np.repeat(np.exp2(scales.astype(np.float64) - 127.0), 8, axis=1)[..., None]
    return vals.transpose(0, 1, 3, 2).reshape(g * 512, n)


def gelu(v):
    return 0.5 * v * (1.0 + np.tanh(np.sqrt(2.0 / np.pi) * (v + 0.044715 * v**3)))


K, T, E, C, N = 512, 1536, 8, 128, 256


def by_expert(wq, xq):
    return np.concatenate([wq[e].T @ xq[:, e * C:(e + 1) * C] for e in range(E)], axis=1)


def setup_inputs():
    n = np.random.standard_normal
    s = mx_kscale(K)[:, None]
    packed = [pack_weight(m) for m in n((E, K, N)) / np.sqrt(K) / s[None]]
    return {
        "xT": (n((K, T)) * s).astype(np.float32),
        "xr": n((N, T)).astype(np.float32),
        "w_words": np.stack([m[0] for m in packed]),
        "w_scales": np.stack([m[1] for m in packed]),
        "b": (0.3 * n((N, E))).astype(np.float32),
        "gate": np.tile(np.random.uniform(0.2, 1.0, E * C), (N, 1)).astype(np.float32),
        "offs": striped(np.random.permutation(T)[:E * C]),
    }


def reference(xT, xr, w_words, w_scales, b, gate, offs):
    idx = unstriped(offs)
    w = np.stack([unpack_weight(w_words[e], w_scales[e]) for e in range(E)])
    xq = mxq(f64(xT)[:, idx], 0, "e4m3")
    y = by_expert(w, xq)
    y = gelu(y + np.repeat(f64(b), C, axis=1))
    out = f64(xr).copy()
    out[:, idx] += f64(gate) * y
    return out

@@ -1,0 +1,129 @@
+from contextlib import ExitStack
+
+import concourse.mybir as mybir
+
+K, T, E, C, N = 512, 1536, 8, 128, 256
+P = 128
+PACK = 4
+S = E * C
+HALVES = N // P
+
+F32 = mybir.dt.float32
+BF16 = mybir.dt.bfloat16
+I32 = mybir.dt.int32
+U32 = mybir.dt.uint32
+U16 = mybir.dt.uint16
+U8 = mybir.dt.uint8
+FP8X4 = mybir.dt.float8_e4m3fn_x4
+ADD = mybir.AluOpType.add
+MULT = mybir.AluOpType.mult
+GELU = mybir.ActivationFunctionType.Gelu_apprx_tanh
+
+FLOPS = 2 * K * N * S
+BYTES = 4 * K * T + 4 * N * T + E * K * N + E * (K // 32) * N + 4 * N * E + 4 * S + 2 * S + 4 * N * T
+
+CHUNKS = [(0, 768), (768, 512), (1280, 256)]
+QUANTISE = 512
+PIECE = 512
+STORES = [[(0, 768), (768, 768)], [(0, 384), (384, 512), (896, 448), (1344, 192)]]
+
+
+def tile_moe_res_lin_gelu_kernel(tc, xT, xr, w_words, w_scales, b, gate, offs, out):
+    nc = tc.nc
+    with ExitStack() as ctx:
+        keep = ctx.enter_context(tc.tile_pool(name="keep", bufs=1))
+        psum = ctx.enter_context(tc.psum_pool(name="psum", bufs=8))
+
+        offsets = keep.tile([P, S // 16], U16, name="offsets")
+        w_codes = keep.tile([P, E * N * PACK], U8, name="w_codes", align_bytes=64)
+        w_planes = keep.tile([P, E * N], U8, name="w_planes", align_bytes=64)
+        bias = [keep.tile([P, E], F32, name=f"bias{h}") for h in range(HALVES)]
+        gates = keep.tile([P, S], F32, name="gates")
+        x_words = keep.tile([P, T], U32, name="x_words", align_bytes=64)
+        x_scales = keep.tile([P, T], U8, name="x_scales", align_bytes=64)
+        warm = keep.tile([P, 1], F32, name="warm")
+        warm_out = keep.tile([P, 1], F32, name="warm_out")
+        landing = [keep.tile([P, T], F32, name=f"landing{h}", align_bytes=64) for h in range(HALVES)]
+        residual = [keep.tile([P, T], F32, name=f"residual{h}", align_bytes=64) for h in range(HALVES)]
+        total = [keep.tile([P, T], F32, name=f"total{h}", align_bytes=64) for h in range(HALVES)]
+
+        nc.vector.memset(w_planes[:].bitcast(I32), 0)
+        nc.gpsimd.memset(x_scales[:], 0)
+        nc.vector.memset(warm[:], 0.0)
+        nc.scalar.activation(warm_out[:], warm[:], GELU)
+        for h in range(HALVES):
+            nc.vector.memset(landing[h][:], 0.0)
+
+        raws = []
+        for i, (t0, width) in enumerate(CHUNKS):
+            raw = keep.tile([P, PACK, width], F32, name=f"raw{i}", align_bytes=64)
+            nc.sync.dma_start(raw[:], xT[:, t0 : t0 + width].rearrange("(p j) t -> p j t", j=PACK))
+            raws.append(raw)
+        nc.sync.dma_start(offsets[:], offs)
+        for q in range(4):
+            nc.sync.dma_start(
+                w_planes[32 * q : 32 * q + 4, :].bitcast(I32).rearrange("q (e n) -> q e n", e=E),
+                w_scales[:, 0, 4 * q : 4 * q + 4, :].rearrange("e q n -> q e n").bitcast(I32),
+            )
+        for e0 in range(0, E, E // 2):
+            nc.sync.dma_start(
+                w_codes[:, e0 * N * PACK : (e0 + E // 2) * N * PACK].bitcast(I32).rearrange("p (e n) -> p e n", e=E // 2),
+                w_words[e0 : e0 + E // 2, 0].rearrange("e p n r -> p e (n r)").bitcast(I32),
+            )
+            if e0 == 0:
+                for h in range(HALVES):
+                    nc.sync.dma_start(bias[h][:], b[h * P : (h + 1) * P, :])
+        nc.sync.dma_start(gates[:], gate[0:P, :])
+        nc.sync.dma_start(residual[1][:], xr[P:N, :])
+        nc.sync.dma_start(residual[0][:], xr[0:P, :])
+
+        for i, (t0, width) in enumerate(CHUNKS):
+            grouped = keep.tile([P, width, PACK], BF16, name=f"grouped{i}", align_bytes=64)
+            cut = width * 3 // 8
+            cut -= cut % 16
+            nc.scalar.copy(grouped[:, 0:cut, :], raws[i][:, :, 0:cut].rearrange("p j t -> p t j"))
+            nc.vector.tensor_copy(grouped[:, cut:width, :], raws[i][:, :, cut:width].rearrange("p j t -> p t j"))
+            for c0 in range(0, width, QUANTISE):
+                c1 = min(c0 + QUANTISE, width)
+                nc.vector.quantize_mx(
+                    out=x_words[:, t0 + c0 : t0 + c1].bitcast(FP8X4),
+                    scales=x_scales[:, t0 + c0 : t0 + c1],
+                    in_=grouped[:, c0:c1, :].rearrange("p t j -> p (t j)"),
+                )
+
+        y = [keep.tile([P, S], F32, name=f"y{h}", align_bytes=64) for h in range(HALVES)]
+        z = [keep.tile([P, S], F32, name=f"z{h}", align_bytes=64) for h in range(HALVES)]
+        for s0 in range(0, S, PIECE):
+            lists = offsets[:, s0 // 16 : (s0 + PIECE) // 16]
+            g_words = keep.tile([P, PIECE], U32, name=f"g_words{s0}", align_bytes=64)
+            g_scales = keep.tile([P, PIECE], U8, name=f"g_scales{s0}", align_bytes=64)
+            nc.vector.tensor_copy(g_words[:], x_words[:].indirect(lists))
+            nc.vector.tensor_copy(g_scales[:], x_scales[:].indirect(lists))
+            for h in range(HALVES):
+                for c0 in range(0, PIECE, C):
+                    e = (s0 + c0) // C
+                    col = e * N + h * P
+                    acc = psum.tile([P, 512], F32, name="acc")
+                    nc.tensor.matmul_mx(
+                        out=acc[:, 0:C],
+                        lhsT=w_codes[:, col * PACK : (col + P) * PACK].bitcast(FP8X4),
+                        lhsT_scale=w_planes[:, col : col + P],
+                        rhs=g_words[:, c0 : c0 + C].bitcast(FP8X4),
+                        rhs_scale=g_scales[:, c0 : c0 + C],
+                        start=True,
+                        stop=True,
+                    )
+                    nc.scalar.activation(y[h][:, e * C : (e + 1) * C], acc[:, 0:C], GELU, bias=bias[h][:, e : e + 1])
+                for c0 in range(s0, s0 + PIECE, 256):
+                    part = slice(c0, c0 + 256)
+                    nc.gpsimd.tensor_tensor(z[h][:, part], y[h][:, part], gates[:, part], MULT)
+
+        for h in range(HALVES):
+            for s0 in range(0, S, PIECE):
+                nc.vector.tensor_copy(landing[h][:].indirect(offsets[:, s0 // 16 : (s0 + PIECE) // 16]), z[h][:, s0 : s0 + PIECE])
+        for h in range(HALVES):
+            adder, queue = (nc.gpsimd, nc.scalar) if h == 0 else (nc.vector, nc.sync)
+            for t0, width in STORES[h]:
+                cols = slice(t0, t0 + width)
+                adder.tensor_tensor(total[h][:, cols], landing[h][:, cols], residual[h][:, cols], ADD)
+                queue.dma_start(out[h * P : (h + 1) * P, cols], total[h][:, cols])

@@ -1,6 +1,7 @@
 from contextlib import ExitStack
 
 import concourse.mybir as mybir
+from concourse.masks import make_identity
 
 K, T, E, C, N = 512, 1536, 8, 128, 256
 P = 128
@@ -18,112 +19,189 @@ FP8X4 = mybir.dt.float8_e4m3fn_x4
 ADD = mybir.AluOpType.add
 MULT = mybir.AluOpType.mult
 GELU = mybir.ActivationFunctionType.Gelu_apprx_tanh
+COPY = mybir.ActivationFunctionType.Copy
 
 FLOPS = 2 * K * N * S
 BYTES = 4 * K * T + 4 * N * T + E * K * N + E * (K // 32) * N + 4 * N * E + 4 * S + 2 * S + 4 * N * T
 
-CHUNKS = [(0, 768), (768, 512), (1280, 256)]
-QUANTISE = 512
-PIECE = 512
-STORES = [[(0, 768), (768, 768)], [(0, 384), (384, 512), (896, 448), (1344, 192)]]
+PAIR_CHUNKS = [(0, 768), (768, 512), (1280, 256)]
+ROW_CHUNKS = [(0, 768), (768, 768)]
+PIECES = [(0, 256), (256, 256), (512, 512)]
+PAIR = 2 * C
+BANK = 512
+SPARE = 16
+STORES = [(0, 256), (256, 512), (768, 512), (1280, 256)]
 
 
 def tile_moe_res_lin_gelu_kernel(tc, xT, xr, w_words, w_scales, b, gate, offs, out):
     nc = tc.nc
     with ExitStack() as ctx:
         keep = ctx.enter_context(tc.tile_pool(name="keep", bufs=1))
-        psum = ctx.enter_context(tc.psum_pool(name="psum", bufs=8))
+        psum = ctx.enter_context(tc.psum_pool(name="psum", bufs=3))
+        turned_banks = ctx.enter_context(tc.psum_pool(name="turned_banks", bufs=3))
+        back_banks = ctx.enter_context(tc.psum_pool(name="back_banks", bufs=2))
 
         offsets = keep.tile([P, S // 16], U16, name="offsets")
-        w_codes = keep.tile([P, E * N * PACK], U8, name="w_codes", align_bytes=64)
+        w_codes = [keep.tile([P, 2 * N * PACK], U8, name=f"w_codes{i}", align_bytes=64) for i in range(E // 2)]
         w_planes = keep.tile([P, E * N], U8, name="w_planes", align_bytes=64)
-        bias = [keep.tile([P, E], F32, name=f"bias{h}") for h in range(HALVES)]
+        bias = keep.tile([P, HALVES, E], F32, name="bias")
         gates = keep.tile([P, S], F32, name="gates")
-        x_words = keep.tile([P, T], U32, name="x_words", align_bytes=64)
-        x_scales = keep.tile([P, T], U8, name="x_scales", align_bytes=64)
+        pair_tile = keep.tile([P, T + PIECES[0][1] * PACK // 2], U32, name="pair_tile", align_bytes=64)
+        pairs = pair_tile[:, 0:T]
+        row2 = keep.tile([P, T], BF16, name="row2", align_bytes=64)
+        row3 = keep.tile([P, T], BF16, name="row3", align_bytes=64)
+        raw2 = keep.tile([P, T], F32, name="raw2", align_bytes=64)
+        raw3 = keep.tile([P, T], F32, name="raw3", align_bytes=64)
         warm = keep.tile([P, 1], F32, name="warm")
         warm_out = keep.tile([P, 1], F32, name="warm_out")
         landing = [keep.tile([P, T], F32, name=f"landing{h}", align_bytes=64) for h in range(HALVES)]
         residual = [keep.tile([P, T], F32, name=f"residual{h}", align_bytes=64) for h in range(HALVES)]
         total = [keep.tile([P, T], F32, name=f"total{h}", align_bytes=64) for h in range(HALVES)]
+        y = [keep.tile([P, S], F32, name=f"y{h}", align_bytes=64) for h in range(HALVES)]
+        grouped = [pair_tile[:, T:].bitcast(BF16)]
+        grouped.extend(keep.tile([P, count * PACK], BF16, name=f"grouped{s0}", align_bytes=64)[:] for s0, count in PIECES[1:])
+        codes = [keep.tile([P, count], U32, name=f"x_codes{s0}", align_bytes=64) for s0, count in PIECES]
+        scales = [keep.tile([P, count], U8, name=f"x_scales{s0}", align_bytes=64) for s0, count in PIECES]
 
+        identity = keep.tile([P, P], F32, name="identity", align_bytes=64)
+        make_identity(nc, identity[:])
         nc.vector.memset(w_planes[:].bitcast(I32), 0)
-        nc.gpsimd.memset(x_scales[:], 0)
         nc.vector.memset(warm[:], 0.0)
         nc.scalar.activation(warm_out[:], warm[:], GELU)
         for h in range(HALVES):
             nc.vector.memset(landing[h][:], 0.0)
 
-        raws = []
-        for i, (t0, width) in enumerate(CHUNKS):
-            raw = keep.tile([P, PACK, width], F32, name=f"raw{i}", align_bytes=64)
-            nc.sync.dma_start(raw[:], xT[:, t0 : t0 + width].rearrange("(p j) t -> p j t", j=PACK))
-            raws.append(raw)
-        nc.sync.dma_start(offsets[:], offs)
+        rows = xT.rearrange("(p j) t -> p j t", j=PACK)
+        for t0, width in ROW_CHUNKS:
+            nc.sync.dma_start(raw2[:, t0 : t0 + width], rows[:, 2, t0 : t0 + width])
+            if t0 == 0:
+                nc.sync.dma_start(offsets[:], offs)
+        raw_pairs = []
+        for i, (t0, width) in enumerate(PAIR_CHUNKS):
+            raw = keep.tile([P, 2, width], F32, name=f"raw_pair{i}", align_bytes=64)
+            nc.sync.dma_start(raw[:], rows[:, 0:2, t0 : t0 + width])
+            raw_pairs.append(raw)
+        for t0, width in ROW_CHUNKS:
+            nc.sync.dma_start(raw3[:, t0 : t0 + width], rows[:, 3, t0 : t0 + width])
         for q in range(4):
             nc.sync.dma_start(
                 w_planes[32 * q : 32 * q + 4, :].bitcast(I32).rearrange("q (e n) -> q e n", e=E),
                 w_scales[:, 0, 4 * q : 4 * q + 4, :].rearrange("e q n -> q e n").bitcast(I32),
             )
-        for e0 in range(0, E, E // 2):
+
+        def load_weights(i):
             nc.sync.dma_start(
-                w_codes[:, e0 * N * PACK : (e0 + E // 2) * N * PACK].bitcast(I32).rearrange("p (e n) -> p e n", e=E // 2),
-                w_words[e0 : e0 + E // 2, 0].rearrange("e p n r -> p e (n r)").bitcast(I32),
+                w_codes[i][:].bitcast(I32).rearrange("p (e n) -> p e n", e=2),
+                w_words[2 * i : 2 * i + 2, 0].rearrange("e p n r -> p e (n r)").bitcast(I32),
             )
-            if e0 == 0:
-                for h in range(HALVES):
-                    nc.sync.dma_start(bias[h][:], b[h * P : (h + 1) * P, :])
-        nc.sync.dma_start(gates[:], gate[0:P, :])
-        nc.sync.dma_start(residual[1][:], xr[P:N, :])
-        nc.sync.dma_start(residual[0][:], xr[0:P, :])
 
-        for i, (t0, width) in enumerate(CHUNKS):
-            grouped = keep.tile([P, width, PACK], BF16, name=f"grouped{i}", align_bytes=64)
-            cut = width * 3 // 8
-            cut -= cut % 16
-            nc.scalar.copy(grouped[:, 0:cut, :], raws[i][:, :, 0:cut].rearrange("p j t -> p t j"))
-            nc.vector.tensor_copy(grouped[:, cut:width, :], raws[i][:, :, cut:width].rearrange("p j t -> p t j"))
-            for c0 in range(0, width, QUANTISE):
-                c1 = min(c0 + QUANTISE, width)
-                nc.vector.quantize_mx(
-                    out=x_words[:, t0 + c0 : t0 + c1].bitcast(FP8X4),
-                    scales=x_scales[:, t0 + c0 : t0 + c1],
-                    in_=grouped[:, c0:c1, :].rearrange("p t j -> p (t j)"),
+        load_weights(0)
+        nc.sync.dma_start(bias[:], b.rearrange("(h p) e -> p h e", p=P))
+        load_weights(1)
+        nc.sync.dma_start(gates[:, 0:PAIR], gate[0:P, 0:PAIR])
+        load_weights(2)
+        load_weights(3)
+        nc.sync.dma_start(gates[:, PAIR:S], gate[0:P, PAIR:S])
+        for h in range(HALVES):
+            nc.sync.dma_start(residual[h][:], xr[h * P : (h + 1) * P, :])
+
+        def lists(s0, count):
+            return offsets[:, s0 // 16 : (s0 + count) // 16]
+
+        def slot_row(i, j):
+            return grouped[i].rearrange("p (s j) -> p s j", j=PACK)[:, :, j]
+
+        def slot_pairs(i):
+            return grouped[i].bitcast(U32).rearrange("p (s u) -> p s u", u=2)[:, :, 0]
+
+        pair_values = pairs.bitcast(BF16).rearrange("p (t j) -> p t j", j=2)
+
+        def cast_row(row, raw):
+            for t0, width in ROW_CHUNKS:
+                nc.scalar.copy(row[:, t0 : t0 + width], raw[:, t0 : t0 + width])
+
+        def gather_row(i, j, row):
+            nc.scalar.activation(slot_row(i, j), row[:].indirect(lists(*PIECES[i])), COPY)
+
+        def quantise(i):
+            nc.vector.quantize_mx(out=codes[i][:].bitcast(FP8X4), scales=scales[i][:], in_=grouped[i])
+
+        def experts(pair, h):
+            acc = psum.tile([P, PAIR], F32, name="acc")
+            for k in range(2):
+                e = 2 * pair + k
+                i = max(n for n, (s0, count) in enumerate(PIECES) if s0 <= e * C)
+                c0 = e * C - PIECES[i][0]
+                col = k * N + h * P
+                nc.tensor.matmul_mx(
+                    out=acc[:, k * C : (k + 1) * C],
+                    lhsT=w_codes[pair][:, col * PACK : (col + P) * PACK].bitcast(FP8X4),
+                    lhsT_scale=w_planes[:, e * N + h * P : e * N + (h + 1) * P],
+                    rhs=codes[i][:, c0 : c0 + C].bitcast(FP8X4),
+                    rhs_scale=scales[i][:, c0 : c0 + C],
+                    start=True,
+                    stop=True,
                 )
+            for k in range(2):
+                e = 2 * pair + k
+                nc.scalar.activation(y[h][:, e * C : (e + 1) * C], acc[:, k * C : (k + 1) * C], GELU, bias=bias[:, h, e : e + 1])
 
-        y = [keep.tile([P, S], F32, name=f"y{h}", align_bytes=64) for h in range(HALVES)]
-        z = [keep.tile([P, S], F32, name=f"z{h}", align_bytes=64) for h in range(HALVES)]
-        for s0 in range(0, S, PIECE):
-            lists = offsets[:, s0 // 16 : (s0 + PIECE) // 16]
-            g_words = keep.tile([P, PIECE], U32, name=f"g_words{s0}", align_bytes=64)
-            g_scales = keep.tile([P, PIECE], U8, name=f"g_scales{s0}", align_bytes=64)
-            nc.vector.tensor_copy(g_words[:], x_words[:].indirect(lists))
-            nc.vector.tensor_copy(g_scales[:], x_scales[:].indirect(lists))
-            for h in range(HALVES):
-                for c0 in range(0, PIECE, C):
-                    e = (s0 + c0) // C
-                    col = e * N + h * P
-                    acc = psum.tile([P, 512], F32, name="acc")
-                    nc.tensor.matmul_mx(
-                        out=acc[:, 0:C],
-                        lhsT=w_codes[:, col * PACK : (col + P) * PACK].bitcast(FP8X4),
-                        lhsT_scale=w_planes[:, col : col + P],
-                        rhs=g_words[:, c0 : c0 + C].bitcast(FP8X4),
-                        rhs_scale=g_scales[:, c0 : c0 + C],
-                        start=True,
-                        stop=True,
-                    )
-                    nc.scalar.activation(y[h][:, e * C : (e + 1) * C], acc[:, 0:C], GELU, bias=bias[h][:, e : e + 1])
-                for c0 in range(s0, s0 + PIECE, 256):
-                    part = slice(c0, c0 + 256)
-                    nc.gpsimd.tensor_tensor(z[h][:, part], y[h][:, part], gates[:, part], MULT)
+        def scatter(s0, count, h):
+            slots = slice(s0, s0 + count)
+            nc.vector.tensor_tensor(landing[h][:].indirect(lists(s0, count)), y[h][:, slots], gates[:, slots], MULT)
 
-        for h in range(HALVES):
-            for s0 in range(0, S, PIECE):
-                nc.vector.tensor_copy(landing[h][:].indirect(offsets[:, s0 // 16 : (s0 + PIECE) // 16]), z[h][:, s0 : s0 + PIECE])
-        for h in range(HALVES):
-            adder, queue = (nc.gpsimd, nc.scalar) if h == 0 else (nc.vector, nc.sync)
-            for t0, width in STORES[h]:
+        def add_and_store(h, queue):
+            for t0, width in STORES:
                 cols = slice(t0, t0 + width)
-                adder.tensor_tensor(total[h][:, cols], landing[h][:, cols], residual[h][:, cols], ADD)
+                nc.vector.tensor_tensor(total[h][:, cols], landing[h][:, cols], residual[h][:, cols], ADD)
                 queue.dma_start(out[h * P : (h + 1) * P, cols], total[h][:, cols])
+
+        def add_by_transposes_and_store(h, queue):
+            banks = []
+            for t0 in range(0, T, BANK):
+                turned = turned_banks.tile([P, BANK], F32, name="turned")
+                for c0 in range(0, BANK, P):
+                    block = residual[h][:, t0 + c0 : t0 + c0 + P]
+                    nc.tensor.matmul(turned[:, c0 : c0 + P], block, identity[:], start=c0 == 0, stop=False, is_transpose=True)
+                banks.append(turned)
+            sums = []
+            for t0, turned in zip(range(0, T, BANK), banks):
+                for c0 in range(0, BANK, P):
+                    block = landing[h][:, t0 + c0 : t0 + c0 + P]
+                    nc.tensor.matmul(turned[:, c0 : c0 + P], block, identity[:], start=False, stop=c0 == BANK - P, is_transpose=True)
+                part = keep.tile([P, BANK], F32, name=f"sums{t0}", align_bytes=64)
+                nc.scalar.copy(part[:], turned[:])
+                sums.append(part)
+            for t0, part in zip(range(0, T, BANK), sums):
+                back = back_banks.tile([P, BANK], F32, name="back")
+                for c0 in range(0, BANK, P):
+                    nc.tensor.transpose(back[:, c0 : c0 + P], part[:, c0 : c0 + P], identity[:])
+                cols = slice(t0, t0 + BANK)
+                nc.scalar.copy(total[h][:, cols], back[:])
+                queue.dma_start(out[h * P : (h + 1) * P, cols], total[h][:, cols])
+
+        nc.vector.tensor_copy(slot_row(0, 2), raw2[:].indirect(lists(*PIECES[0])))
+        cast_row(row2, raw2)
+        for i in range(1, len(PIECES)):
+            gather_row(i, 2, row2)
+        for raw, (t0, width) in zip(raw_pairs, PAIR_CHUNKS):
+            nc.vector.tensor_copy(pair_values[:, t0 : t0 + width, :], raw[:].rearrange("p j t -> p t j"))
+        for i in range(2):
+            nc.vector.tensor_copy(slot_pairs(i), pairs.indirect(lists(*PIECES[i])))
+        nc.vector.tensor_copy(slot_row(0, 3), raw3[:].indirect(lists(*PIECES[0])))
+        quantise(0)
+        cast_row(row3, raw3)
+        nc.vector.tensor_copy(slot_pairs(2), pair_tile[:, 0 : T + SPARE].indirect(lists(*PIECES[2])))
+        for i in range(1, len(PIECES)):
+            gather_row(i, 3, row3)
+            quantise(i)
+        experts(0, 0)
+        scatter(0, PAIR, 0)
+        for pair in range(1, E // 2):
+            experts(pair, 0)
+        scatter(PAIR, S - PAIR, 0)
+        for pair in range(E // 2):
+            experts(pair, 1)
+        scatter(0, S, 1)
+        add_by_transposes_and_store(0, nc.scalar)
+        add_and_store(1, nc.sync)

@@ -26,7 +26,8 @@ BYTES = 4 * K * T + 4 * N * T + E * K * N + E * (K // 32) * N + 4 * N * E + 4 * 
 
 PAIR_CHUNKS = [(0, 768), (768, 512), (1280, 256)]
 ROW_CHUNKS = [(0, 768), (768, 768)]
-PIECES = [(0, 256), (256, 256), (512, 512)]
+LAST_ROW_CHUNKS = [(1024, 512), (512, 512), (0, 512)]
+PIECES = [(0, 256), (256, 256), (512, 256), (768, 256)]
 PAIR = 2 * C
 BANK = 512
 SPARE = 16
@@ -46,20 +47,19 @@ def tile_moe_res_lin_gelu_kernel(tc, xT, xr, w_words, w_scales, b, gate, offs, o
         w_planes = keep.tile([P, E * N], U8, name="w_planes", align_bytes=64)
         bias = keep.tile([P, HALVES, E], F32, name="bias")
         gates = keep.tile([P, S], F32, name="gates")
-        pair_tile = keep.tile([P, T + PIECES[0][1] * PACK // 2], U32, name="pair_tile", align_bytes=64)
+        pair_tile = keep.tile([P, 2 * T], U32, name="pair_tile", align_bytes=64)
         pairs = pair_tile[:, 0:T]
         row2 = keep.tile([P, T], BF16, name="row2", align_bytes=64)
         row3 = keep.tile([P, T], BF16, name="row3", align_bytes=64)
         raw2 = keep.tile([P, T], F32, name="raw2", align_bytes=64)
-        raw3 = keep.tile([P, T], F32, name="raw3", align_bytes=64)
+        raw3 = pair_tile[:, T:].bitcast(F32)
         warm = keep.tile([P, 1], F32, name="warm")
         warm_out = keep.tile([P, 1], F32, name="warm_out")
         landing = [keep.tile([P, T], F32, name=f"landing{h}", align_bytes=64) for h in range(HALVES)]
         residual = [keep.tile([P, T], F32, name=f"residual{h}", align_bytes=64) for h in range(HALVES)]
         total = [keep.tile([P, T], F32, name=f"total{h}", align_bytes=64) for h in range(HALVES)]
         y = [keep.tile([P, S], F32, name=f"y{h}", align_bytes=64) for h in range(HALVES)]
-        grouped = [pair_tile[:, T:].bitcast(BF16)]
-        grouped.extend(keep.tile([P, count * PACK], BF16, name=f"grouped{s0}", align_bytes=64)[:] for s0, count in PIECES[1:])
+        grouped = [keep.tile([P, count * PACK], BF16, name=f"grouped{s0}", align_bytes=64)[:] for s0, count in PIECES]
         codes = [keep.tile([P, count], U32, name=f"x_codes{s0}", align_bytes=64) for s0, count in PIECES]
         scales = [keep.tile([P, count], U8, name=f"x_scales{s0}", align_bytes=64) for s0, count in PIECES]
 
@@ -81,7 +81,7 @@ def tile_moe_res_lin_gelu_kernel(tc, xT, xr, w_words, w_scales, b, gate, offs, o
             raw = keep.tile([P, 2, width], F32, name=f"raw_pair{i}", align_bytes=64)
             nc.sync.dma_start(raw[:], rows[:, 0:2, t0 : t0 + width])
             raw_pairs.append(raw)
-        for t0, width in ROW_CHUNKS:
+        for t0, width in LAST_ROW_CHUNKS:
             nc.sync.dma_start(raw3[:, t0 : t0 + width], rows[:, 3, t0 : t0 + width])
         for q in range(4):
             nc.sync.dma_start(
@@ -116,8 +116,8 @@ def tile_moe_res_lin_gelu_kernel(tc, xT, xr, w_words, w_scales, b, gate, offs, o
 
         pair_values = pairs.bitcast(BF16).rearrange("p (t j) -> p t j", j=2)
 
-        def cast_row(row, raw):
-            for t0, width in ROW_CHUNKS:
+        def cast_row(row, raw, chunks):
+            for t0, width in chunks:
                 nc.scalar.copy(row[:, t0 : t0 + width], raw[:, t0 : t0 + width])
 
         def gather_row(i, j, row):
@@ -181,27 +181,29 @@ def tile_moe_res_lin_gelu_kernel(tc, xT, xr, w_words, w_scales, b, gate, offs, o
                 queue.dma_start(out[h * P : (h + 1) * P, cols], total[h][:, cols])
 
         nc.vector.tensor_copy(slot_row(0, 2), raw2[:].indirect(lists(*PIECES[0])))
-        cast_row(row2, raw2)
+        cast_row(row2, raw2, ROW_CHUNKS)
         for i in range(1, len(PIECES)):
             gather_row(i, 2, row2)
         for raw, (t0, width) in zip(raw_pairs, PAIR_CHUNKS):
             nc.vector.tensor_copy(pair_values[:, t0 : t0 + width, :], raw[:].rearrange("p j t -> p t j"))
         for i in range(2):
             nc.vector.tensor_copy(slot_pairs(i), pairs.indirect(lists(*PIECES[i])))
-        nc.vector.tensor_copy(slot_row(0, 3), raw3[:].indirect(lists(*PIECES[0])))
-        quantise(0)
-        cast_row(row3, raw3)
-        nc.vector.tensor_copy(slot_pairs(2), pair_tile[:, 0 : T + SPARE].indirect(lists(*PIECES[2])))
+        nc.vector.tensor_copy(slot_row(0, 3), raw3.indirect(lists(*PIECES[0])))
+        cast_row(row3, raw3, LAST_ROW_CHUNKS)
+        for i in range(2):
+            nc.vector.tensor_copy(slot_pairs(2 + i), pair_tile[:, 0 : T + SPARE].indirect(lists(*PIECES[2 + i])))
+            if i == 0:
+                quantise(0)
         for i in range(1, len(PIECES)):
             gather_row(i, 3, row3)
             quantise(i)
-        experts(0, 0)
-        scatter(0, PAIR, 0)
-        for pair in range(1, E // 2):
-            experts(pair, 0)
-        scatter(PAIR, S - PAIR, 0)
+        experts(0, 1)
+        scatter(0, PAIR, 1)
         for pair in range(E // 2):
+            experts(pair, 0)
+        scatter(0, S, 0)
+        for pair in range(1, E // 2):
             experts(pair, 1)
-        scatter(0, S, 1)
+        scatter(PAIR, S - PAIR, 1)
         add_by_transposes_and_store(0, nc.scalar)
         add_and_store(1, nc.sync)

@@ -26,8 +26,9 @@ BYTES = 4 * K * T + 4 * N * T + E * K * N + E * (K // 32) * N + 4 * N * E + 4 * 
 
 PAIR_CHUNKS = [(0, 768), (768, 512), (1280, 256)]
 ROW_CHUNKS = [(0, 768), (768, 768)]
-LAST_ROW_CHUNKS = [(1024, 512), (512, 512), (0, 512)]
-PIECES = [(0, 256), (256, 256), (512, 256), (768, 256)]
+LAST_ROW_CHUNKS = [(768, 768), (0, 768)]
+GROUP = 512
+PIECE = 256
 PAIR = 2 * C
 BANK = 512
 SPARE = 16
@@ -56,20 +57,22 @@ def tile_moe_res_lin_gelu_kernel(tc, xT, xr, w_words, w_scales, b, gate, offs, o
         warm = keep.tile([P, 1], F32, name="warm")
         warm_out = keep.tile([P, 1], F32, name="warm_out")
         landing = [keep.tile([P, T], F32, name=f"landing{h}", align_bytes=64) for h in range(HALVES)]
+        first_landing = keep.tile([P, T], F32, name="first_landing", align_bytes=64)
         residual = [keep.tile([P, T], F32, name=f"residual{h}", align_bytes=64) for h in range(HALVES)]
         total = [keep.tile([P, T], F32, name=f"total{h}", align_bytes=64) for h in range(HALVES)]
         y = [keep.tile([P, S], F32, name=f"y{h}", align_bytes=64) for h in range(HALVES)]
-        grouped = [keep.tile([P, count * PACK], BF16, name=f"grouped{s0}", align_bytes=64)[:] for s0, count in PIECES]
-        codes = [keep.tile([P, count], U32, name=f"x_codes{s0}", align_bytes=64) for s0, count in PIECES]
-        scales = [keep.tile([P, count], U8, name=f"x_scales{s0}", align_bytes=64) for s0, count in PIECES]
+        grouped = [keep.tile([P, GROUP * PACK], BF16, name=f"grouped{g}", align_bytes=64) for g in range(S // GROUP)]
+        codes = [keep.tile([P, GROUP], U32, name=f"x_codes{g}", align_bytes=64) for g in range(S // GROUP)]
+        scales = [keep.tile([P, GROUP], U8, name=f"x_scales{g}", align_bytes=64) for g in range(S // GROUP)]
 
         identity = keep.tile([P, P], F32, name="identity", align_bytes=64)
         make_identity(nc, identity[:])
         nc.vector.memset(w_planes[:].bitcast(I32), 0)
         nc.vector.memset(warm[:], 0.0)
         nc.scalar.activation(warm_out[:], warm[:], GELU)
-        for h in range(HALVES):
-            nc.vector.memset(landing[h][:], 0.0)
+        for window in (first_landing, landing[0]):
+            nc.vector.memset(window[:], 0.0)
+        nc.gpsimd.memset(landing[1][:], 0.0)
 
         rows = xT.rearrange("(p j) t -> p j t", j=PACK)
         for t0, width in ROW_CHUNKS:
@@ -108,11 +111,12 @@ def tile_moe_res_lin_gelu_kernel(tc, xT, xr, w_words, w_scales, b, gate, offs, o
         def lists(s0, count):
             return offsets[:, s0 // 16 : (s0 + count) // 16]
 
-        def slot_row(i, j):
-            return grouped[i].rearrange("p (s j) -> p s j", j=PACK)[:, :, j]
+        def slot_row(s0, count, j):
+            c0 = s0 % GROUP
+            return grouped[s0 // GROUP][:].rearrange("p (s j) -> p s j", j=PACK)[:, c0 : c0 + count, j]
 
-        def slot_pairs(i):
-            return grouped[i].bitcast(U32).rearrange("p (s u) -> p s u", u=2)[:, :, 0]
+        def slot_pairs(g):
+            return grouped[g][:].bitcast(U32).rearrange("p (s u) -> p s u", u=2)[:, :, 0]
 
         pair_values = pairs.bitcast(BF16).rearrange("p (t j) -> p t j", j=2)
 
@@ -120,18 +124,22 @@ def tile_moe_res_lin_gelu_kernel(tc, xT, xr, w_words, w_scales, b, gate, offs, o
             for t0, width in chunks:
                 nc.scalar.copy(row[:, t0 : t0 + width], raw[:, t0 : t0 + width])
 
-        def gather_row(i, j, row):
-            nc.scalar.activation(slot_row(i, j), row[:].indirect(lists(*PIECES[i])), COPY)
+        def gather_row(s0, count, j, row):
+            nc.scalar.activation(slot_row(s0, count, j), row[:].indirect(lists(s0, count)), COPY)
 
-        def quantise(i):
-            nc.vector.quantize_mx(out=codes[i][:].bitcast(FP8X4), scales=scales[i][:], in_=grouped[i])
+        def quantise(s0, count):
+            g, c0 = divmod(s0, GROUP)
+            nc.vector.quantize_mx(
+                out=codes[g][:, c0 : c0 + count].bitcast(FP8X4),
+                scales=scales[g][:, c0 : c0 + count],
+                in_=grouped[g][:, c0 * PACK : (c0 + count) * PACK],
+            )
 
         def experts(pair, h):
             acc = psum.tile([P, PAIR], F32, name="acc")
             for k in range(2):
                 e = 2 * pair + k
-                i = max(n for n, (s0, count) in enumerate(PIECES) if s0 <= e * C)
-                c0 = e * C - PIECES[i][0]
+                i, c0 = divmod(e * C, GROUP)
                 col = k * N + h * P
                 nc.tensor.matmul_mx(
                     out=acc[:, k * C : (k + 1) * C],
@@ -146,9 +154,9 @@ def tile_moe_res_lin_gelu_kernel(tc, xT, xr, w_words, w_scales, b, gate, offs, o
                 e = 2 * pair + k
                 nc.scalar.activation(y[h][:, e * C : (e + 1) * C], acc[:, k * C : (k + 1) * C], GELU, bias=bias[:, h, e : e + 1])
 
-        def scatter(s0, count, h):
+        def scatter(window, s0, count, h):
             slots = slice(s0, s0 + count)
-            nc.vector.tensor_tensor(landing[h][:].indirect(lists(s0, count)), y[h][:, slots], gates[:, slots], MULT)
+            nc.vector.tensor_tensor(window[:].indirect(lists(s0, count)), y[h][:, slots], gates[:, slots], MULT)
 
         def add_and_store(h, queue):
             for t0, width in STORES:
@@ -164,6 +172,10 @@ def tile_moe_res_lin_gelu_kernel(tc, xT, xr, w_words, w_scales, b, gate, offs, o
                     block = residual[h][:, t0 + c0 : t0 + c0 + P]
                     nc.tensor.matmul(turned[:, c0 : c0 + P], block, identity[:], start=c0 == 0, stop=False, is_transpose=True)
                 banks.append(turned)
+            for t0, turned in zip(range(0, T, BANK), banks):
+                for c0 in range(0, BANK, P):
+                    block = first_landing[:, t0 + c0 : t0 + c0 + P]
+                    nc.tensor.matmul(turned[:, c0 : c0 + P], block, identity[:], start=False, stop=False, is_transpose=True)
             sums = []
             for t0, turned in zip(range(0, T, BANK), banks):
                 for c0 in range(0, BANK, P):
@@ -180,30 +192,28 @@ def tile_moe_res_lin_gelu_kernel(tc, xT, xr, w_words, w_scales, b, gate, offs, o
                 nc.scalar.copy(total[h][:, cols], back[:])
                 queue.dma_start(out[h * P : (h + 1) * P, cols], total[h][:, cols])
 
-        nc.vector.tensor_copy(slot_row(0, 2), raw2[:].indirect(lists(*PIECES[0])))
+        nc.vector.tensor_copy(slot_row(0, PIECE, 2), raw2[:].indirect(lists(0, PIECE)))
         cast_row(row2, raw2, ROW_CHUNKS)
-        for i in range(1, len(PIECES)):
-            gather_row(i, 2, row2)
+        gather_row(PIECE, PIECE, 2, row2)
+        gather_row(GROUP, GROUP, 2, row2)
         for raw, (t0, width) in zip(raw_pairs, PAIR_CHUNKS):
             nc.vector.tensor_copy(pair_values[:, t0 : t0 + width, :], raw[:].rearrange("p j t -> p t j"))
-        for i in range(2):
-            nc.vector.tensor_copy(slot_pairs(i), pairs.indirect(lists(*PIECES[i])))
-        nc.vector.tensor_copy(slot_row(0, 3), raw3.indirect(lists(*PIECES[0])))
+        nc.vector.tensor_copy(slot_pairs(0), pairs.indirect(lists(0, GROUP)))
+        nc.vector.tensor_copy(slot_row(0, PIECE, 3), raw3.indirect(lists(0, PIECE)))
+        nc.vector.tensor_copy(slot_pairs(1), pair_tile[:, 0 : T + SPARE].indirect(lists(GROUP, GROUP)))
         cast_row(row3, raw3, LAST_ROW_CHUNKS)
-        for i in range(2):
-            nc.vector.tensor_copy(slot_pairs(2 + i), pair_tile[:, 0 : T + SPARE].indirect(lists(*PIECES[2 + i])))
-            if i == 0:
-                quantise(0)
-        for i in range(1, len(PIECES)):
-            gather_row(i, 3, row3)
-            quantise(i)
-        experts(0, 1)
-        scatter(0, PAIR, 1)
-        for pair in range(E // 2):
-            experts(pair, 0)
-        scatter(0, S, 0)
+        for s0 in range(PIECE, S, PIECE):
+            gather_row(s0, PIECE, 3, row3)
+        quantise(0, GROUP)
+        for s0 in range(GROUP, S, PIECE):
+            quantise(s0, PIECE)
+        experts(0, 0)
+        scatter(first_landing, 0, PAIR, 0)
         for pair in range(1, E // 2):
+            experts(pair, 0)
+        scatter(landing[0], PAIR, S - PAIR, 0)
+        for pair in range(E // 2):
             experts(pair, 1)
-        scatter(PAIR, S - PAIR, 1)
+        scatter(landing[1], 0, S, 1)
         add_by_transposes_and_store(0, nc.scalar)
         add_and_store(1, nc.sync)

@@ -32,6 +32,7 @@ PIECE = 256
 PAIR = 2 * C
 BANK = 512
 SPARE = 16
+PLANES = 4
 STORES = [(0, 256), (256, 512), (768, 512), (1280, 256)]
 
 
@@ -45,7 +46,7 @@ def tile_moe_res_lin_gelu_kernel(tc, xT, xr, w_words, w_scales, b, gate, offs, o
 
         offsets = keep.tile([P, S // 16], U16, name="offsets")
         w_codes = [keep.tile([P, 2 * N * PACK], U8, name=f"w_codes{i}", align_bytes=64) for i in range(E // 2)]
-        w_planes = keep.tile([P, E * N], U8, name="w_planes", align_bytes=64)
+        w_planes = [keep.tile([P, N], U8, name=f"w_planes{g}", align_bytes=64) for g in range(E // PLANES)]
         bias = keep.tile([P, HALVES, E], F32, name="bias")
         gates = keep.tile([P, S], F32, name="gates")
         pair_tile = keep.tile([P, 2 * T], U32, name="pair_tile", align_bytes=64)
@@ -67,7 +68,8 @@ def tile_moe_res_lin_gelu_kernel(tc, xT, xr, w_words, w_scales, b, gate, offs, o
 
         identity = keep.tile([P, P], F32, name="identity", align_bytes=64)
         make_identity(nc, identity[:])
-        nc.vector.memset(w_planes[:].bitcast(I32), 0)
+        for planes in w_planes:
+            nc.vector.memset(planes[:].bitcast(I32), 0)
         nc.vector.memset(warm[:], 0.0)
         nc.scalar.activation(warm_out[:], warm[:], GELU)
         for window in (first_landing, landing[0]):
@@ -86,11 +88,13 @@ def tile_moe_res_lin_gelu_kernel(tc, xT, xr, w_words, w_scales, b, gate, offs, o
             raw_pairs.append(raw)
         for t0, width in LAST_ROW_CHUNKS:
             nc.sync.dma_start(raw3[:, t0 : t0 + width], rows[:, 3, t0 : t0 + width])
-        for q in range(4):
-            nc.sync.dma_start(
-                w_planes[32 * q : 32 * q + 4, :].bitcast(I32).rearrange("q (e n) -> q e n", e=E),
-                w_scales[:, 0, 4 * q : 4 * q + 4, :].rearrange("e q n -> q e n").bitcast(I32),
-            )
+
+        def load_scales(g):
+            for q in range(4):
+                nc.sync.dma_start(
+                    w_planes[g][32 * q : 32 * q + 4 * PLANES, :].bitcast(I32),
+                    w_scales[PLANES * g : PLANES * (g + 1), 0, 4 * q : 4 * q + 4, :].bitcast(I32),
+                )
 
         def load_weights(i):
             nc.sync.dma_start(
@@ -98,15 +102,17 @@ def tile_moe_res_lin_gelu_kernel(tc, xT, xr, w_words, w_scales, b, gate, offs, o
                 w_words[2 * i : 2 * i + 2, 0].rearrange("e p n r -> p e (n r)").bitcast(I32),
             )
 
+        load_scales(0)
         load_weights(0)
         nc.sync.dma_start(bias[:], b.rearrange("(h p) e -> p h e", p=P))
         load_weights(1)
-        nc.sync.dma_start(gates[:, 0:PAIR], gate[0:P, 0:PAIR])
+        nc.sync.dma_start(gates[:, 0:GROUP], gate[0:P, 0:GROUP])
+        load_scales(1)
         load_weights(2)
         load_weights(3)
-        nc.sync.dma_start(gates[:, PAIR:S], gate[0:P, PAIR:S])
-        for h in range(HALVES):
-            nc.sync.dma_start(residual[h][:], xr[h * P : (h + 1) * P, :])
+        nc.sync.dma_start(residual[0][:], xr[0:P, :])
+        nc.sync.dma_start(gates[:, GROUP:S], gate[0:P, GROUP:S])
+        nc.sync.dma_start(residual[1][:], xr[P:N, :])
 
         def lists(s0, count):
             return offsets[:, s0 // 16 : (s0 + count) // 16]
@@ -144,7 +150,7 @@ def tile_moe_res_lin_gelu_kernel(tc, xT, xr, w_words, w_scales, b, gate, offs, o
                 nc.tensor.matmul_mx(
                     out=acc[:, k * C : (k + 1) * C],
                     lhsT=w_codes[pair][:, col * PACK : (col + P) * PACK].bitcast(FP8X4),
-                    lhsT_scale=w_planes[:, e * N + h * P : e * N + (h + 1) * P],
+                    lhsT_scale=w_planes[e // PLANES][4 * (e % PLANES) : P, h * P : (h + 1) * P],
                     rhs=codes[i][:, c0 : c0 + C].bitcast(FP8X4),
                     rhs_scale=scales[i][:, c0 : c0 + C],
                     start=True,
@@ -204,14 +210,15 @@ def tile_moe_res_lin_gelu_kernel(tc, xT, xr, w_words, w_scales, b, gate, offs, o
         cast_row(row3, raw3, LAST_ROW_CHUNKS)
         for s0 in range(PIECE, S, PIECE):
             gather_row(s0, PIECE, 3, row3)
-        quantise(0, GROUP)
-        for s0 in range(GROUP, S, PIECE):
+        for s0 in range(0, S, PIECE):
             quantise(s0, PIECE)
         experts(0, 0)
-        scatter(first_landing, 0, PAIR, 0)
-        for pair in range(1, E // 2):
+        scatter(landing[0], 0, PAIR, 0)
+        experts(1, 0)
+        scatter(first_landing, PAIR, PAIR, 0)
+        for pair in range(2, E // 2):
             experts(pair, 0)
-        scatter(landing[0], PAIR, S - PAIR, 0)
+        scatter(landing[0], GROUP, GROUP, 0)
         for pair in range(E // 2):
             experts(pair, 1)
         scatter(landing[1], 0, S, 1)

@@ -26,9 +26,10 @@ BYTES = 4 * K * T + 4 * N * T + E * K * N + E * (K // 32) * N + 4 * N * E + 4 * 
 
 PAIR_CHUNKS = [(0, 768), (768, 512), (1280, 256)]
 ROW_CHUNKS = [(0, 768), (768, 768)]
-LAST_ROW_CHUNKS = [(768, 768), (0, 768)]
+LAST_ROW_CHUNKS = [(1024, 512), (512, 512), (0, 512)]
 GROUP = 512
 PIECE = 256
+VECTOR_SLOTS = 192
 PAIR = 2 * C
 BANK = 512
 SPARE = 16
@@ -198,17 +199,18 @@ def tile_moe_res_lin_gelu_kernel(tc, xT, xr, w_words, w_scales, b, gate, offs, o
                 nc.scalar.copy(total[h][:, cols], back[:])
                 queue.dma_start(out[h * P : (h + 1) * P, cols], total[h][:, cols])
 
-        nc.vector.tensor_copy(slot_row(0, PIECE, 2), raw2[:].indirect(lists(0, PIECE)))
+        nc.vector.tensor_copy(slot_row(0, VECTOR_SLOTS, 2), raw2[:].indirect(lists(0, VECTOR_SLOTS)))
         cast_row(row2, raw2, ROW_CHUNKS)
-        gather_row(PIECE, PIECE, 2, row2)
+        gather_row(VECTOR_SLOTS, GROUP - VECTOR_SLOTS, 2, row2)
         gather_row(GROUP, GROUP, 2, row2)
         for raw, (t0, width) in zip(raw_pairs, PAIR_CHUNKS):
             nc.vector.tensor_copy(pair_values[:, t0 : t0 + width, :], raw[:].rearrange("p j t -> p t j"))
         nc.vector.tensor_copy(slot_pairs(0), pairs.indirect(lists(0, GROUP)))
-        nc.vector.tensor_copy(slot_row(0, PIECE, 3), raw3.indirect(lists(0, PIECE)))
+        nc.vector.tensor_copy(slot_row(0, VECTOR_SLOTS, 3), raw3.indirect(lists(0, VECTOR_SLOTS)))
         nc.vector.tensor_copy(slot_pairs(1), pair_tile[:, 0 : T + SPARE].indirect(lists(GROUP, GROUP)))
         cast_row(row3, raw3, LAST_ROW_CHUNKS)
-        for s0 in range(PIECE, S, PIECE):
+        gather_row(VECTOR_SLOTS, GROUP - VECTOR_SLOTS, 3, row3)
+        for s0 in range(GROUP, S, PIECE):
             gather_row(s0, PIECE, 3, row3)
         for s0 in range(0, S, PIECE):
             quantise(s0, PIECE)

@@ -25,8 +25,7 @@ FLOPS = 2 * K * N * S
 BYTES = 4 * K * T + 4 * N * T + E * K * N + E * (K // 32) * N + 4 * N * E + 4 * S + 2 * S + 4 * N * T
 
 PAIR_CHUNKS = [(0, 768), (768, 512), (1280, 256)]
-ROW_CHUNKS = [(0, 768), (768, 768)]
-LAST_ROW_CHUNKS = [(1024, 512), (512, 512), (0, 512)]
+LAST_ROW_CHUNKS = [(1088, 448), (640, 448), (256, 384), (0, 256)]
 GROUP = 512
 PIECE = 256
 VECTOR_SLOTS = 192
@@ -78,10 +77,8 @@ def tile_moe_res_lin_gelu_kernel(tc, xT, xr, w_words, w_scales, b, gate, offs, o
         nc.gpsimd.memset(landing[1][:], 0.0)
 
         rows = xT.rearrange("(p j) t -> p j t", j=PACK)
-        for t0, width in ROW_CHUNKS:
-            nc.sync.dma_start(raw2[:, t0 : t0 + width], rows[:, 2, t0 : t0 + width])
-            if t0 == 0:
-                nc.sync.dma_start(offsets[:], offs)
+        nc.sync.dma_start(raw2[:], rows[:, 2, :])
+        nc.sync.dma_start(offsets[:], offs)
         raw_pairs = []
         for i, (t0, width) in enumerate(PAIR_CHUNKS):
             raw = keep.tile([P, 2, width], F32, name=f"raw_pair{i}", align_bytes=64)
@@ -199,8 +196,8 @@ def tile_moe_res_lin_gelu_kernel(tc, xT, xr, w_words, w_scales, b, gate, offs, o
                 nc.scalar.copy(total[h][:, cols], back[:])
                 queue.dma_start(out[h * P : (h + 1) * P, cols], total[h][:, cols])
 
+        nc.vector.tensor_copy(row2[:], raw2[:])
         nc.vector.tensor_copy(slot_row(0, VECTOR_SLOTS, 2), raw2[:].indirect(lists(0, VECTOR_SLOTS)))
-        cast_row(row2, raw2, ROW_CHUNKS)
         gather_row(VECTOR_SLOTS, GROUP - VECTOR_SLOTS, 2, row2)
         gather_row(GROUP, GROUP, 2, row2)
         for raw, (t0, width) in zip(raw_pairs, PAIR_CHUNKS):

@@ -24,14 +24,12 @@ COPY = mybir.ActivationFunctionType.Copy
 FLOPS = 2 * K * N * S
 BYTES = 4 * K * T + 4 * N * T + E * K * N + E * (K // 32) * N + 4 * N * E + 4 * S + 2 * S + 4 * N * T
 
-PAIR_CHUNKS = [(0, 768), (768, 512), (1280, 256)]
-LAST_ROW_CHUNKS = [(1088, 448), (640, 448), (256, 384), (0, 256)]
+ROW_LOADS = [2, 2, 2, 3]
+VECTOR_SLOTS = 576
 GROUP = 512
 PIECE = 256
-VECTOR_SLOTS = 192
 PAIR = 2 * C
 BANK = 512
-SPARE = 16
 PLANES = 4
 STORES = [(0, 256), (256, 512), (768, 512), (1280, 256)]
 
@@ -49,20 +47,15 @@ def tile_moe_res_lin_gelu_kernel(tc, xT, xr, w_words, w_scales, b, gate, offs, o
         w_planes = [keep.tile([P, N], U8, name=f"w_planes{g}", align_bytes=64) for g in range(E // PLANES)]
         bias = keep.tile([P, HALVES, E], F32, name="bias")
         gates = keep.tile([P, S], F32, name="gates")
-        pair_tile = keep.tile([P, 2 * T], U32, name="pair_tile", align_bytes=64)
-        pairs = pair_tile[:, 0:T]
-        row2 = keep.tile([P, T], BF16, name="row2", align_bytes=64)
-        row3 = keep.tile([P, T], BF16, name="row3", align_bytes=64)
-        raw2 = keep.tile([P, T], F32, name="raw2", align_bytes=64)
-        raw3 = pair_tile[:, T:].bitcast(F32)
+        raw = [keep.tile([P, T], F32, name=f"raw{j}", align_bytes=64) for j in range(PACK)]
+        rounded = [keep.tile([P, T], BF16, name=f"rounded{j}", align_bytes=64) for j in range(PACK)]
         warm = keep.tile([P, 1], F32, name="warm")
         warm_out = keep.tile([P, 1], F32, name="warm_out")
-        landing = [keep.tile([P, T], F32, name=f"landing{h}", align_bytes=64) for h in range(HALVES)]
-        first_landing = keep.tile([P, T], F32, name="first_landing", align_bytes=64)
+        windows = [keep.tile([P, T], F32, name=f"window{i}", align_bytes=64) for i in range(2)]
         residual = [keep.tile([P, T], F32, name=f"residual{h}", align_bytes=64) for h in range(HALVES)]
         total = [keep.tile([P, T], F32, name=f"total{h}", align_bytes=64) for h in range(HALVES)]
         y = [keep.tile([P, S], F32, name=f"y{h}", align_bytes=64) for h in range(HALVES)]
-        grouped = [keep.tile([P, GROUP * PACK], BF16, name=f"grouped{g}", align_bytes=64) for g in range(S // GROUP)]
+        grouped = keep.tile([P, S * PACK], BF16, name="grouped", tag="slots_then_window", align_bytes=64)
         codes = [keep.tile([P, GROUP], U32, name=f"x_codes{g}", align_bytes=64) for g in range(S // GROUP)]
         scales = [keep.tile([P, GROUP], U8, name=f"x_scales{g}", align_bytes=64) for g in range(S // GROUP)]
 
@@ -72,20 +65,20 @@ def tile_moe_res_lin_gelu_kernel(tc, xT, xr, w_words, w_scales, b, gate, offs, o
             nc.vector.memset(planes[:].bitcast(I32), 0)
         nc.vector.memset(warm[:], 0.0)
         nc.scalar.activation(warm_out[:], warm[:], GELU)
-        for window in (first_landing, landing[0]):
+        for window in windows:
             nc.vector.memset(window[:], 0.0)
-        nc.gpsimd.memset(landing[1][:], 0.0)
 
         rows = xT.rearrange("(p j) t -> p j t", j=PACK)
-        nc.sync.dma_start(raw2[:], rows[:, 2, :])
-        nc.sync.dma_start(offsets[:], offs)
-        raw_pairs = []
-        for i, (t0, width) in enumerate(PAIR_CHUNKS):
-            raw = keep.tile([P, 2, width], F32, name=f"raw_pair{i}", align_bytes=64)
-            nc.sync.dma_start(raw[:], rows[:, 0:2, t0 : t0 + width])
-            raw_pairs.append(raw)
-        for t0, width in LAST_ROW_CHUNKS:
-            nc.sync.dma_start(raw3[:, t0 : t0 + width], rows[:, 3, t0 : t0 + width])
+
+        def chunks(j):
+            width = T // ROW_LOADS[j]
+            return [slice(t0, t0 + width) for t0 in range(0, T, width)]
+
+        for j in range(PACK):
+            for cols in chunks(j):
+                nc.sync.dma_start(raw[j][:, cols], rows[:, j, cols])
+                if j == 0 and cols.start == 0:
+                    nc.sync.dma_start(offsets[:], offs)
 
         def load_scales(g):
             for q in range(4):
@@ -116,27 +109,17 @@ def tile_moe_res_lin_gelu_kernel(tc, xT, xr, w_words, w_scales, b, gate, offs, o
             return offsets[:, s0 // 16 : (s0 + count) // 16]
 
         def slot_row(s0, count, j):
-            c0 = s0 % GROUP
-            return grouped[s0 // GROUP][:].rearrange("p (s j) -> p s j", j=PACK)[:, c0 : c0 + count, j]
+            return grouped[:].rearrange("p (s j) -> p s j", j=PACK)[:, s0 : s0 + count, j]
 
-        def slot_pairs(g):
-            return grouped[g][:].bitcast(U32).rearrange("p (s u) -> p s u", u=2)[:, :, 0]
-
-        pair_values = pairs.bitcast(BF16).rearrange("p (t j) -> p t j", j=2)
-
-        def cast_row(row, raw, chunks):
-            for t0, width in chunks:
-                nc.scalar.copy(row[:, t0 : t0 + width], raw[:, t0 : t0 + width])
-
-        def gather_row(s0, count, j, row):
-            nc.scalar.activation(slot_row(s0, count, j), row[:].indirect(lists(s0, count)), COPY)
+        def pieces(s0, cut, s1):
+            return [(a, z) for a, z in ((s0, cut), (cut, s1)) if z > a]
 
         def quantise(s0, count):
             g, c0 = divmod(s0, GROUP)
             nc.vector.quantize_mx(
                 out=codes[g][:, c0 : c0 + count].bitcast(FP8X4),
                 scales=scales[g][:, c0 : c0 + count],
-                in_=grouped[g][:, c0 * PACK : (c0 + count) * PACK],
+                in_=grouped[:, s0 * PACK : (s0 + count) * PACK],
             )
 
         def experts(pair, h):
@@ -162,32 +145,31 @@ def tile_moe_res_lin_gelu_kernel(tc, xT, xr, w_words, w_scales, b, gate, offs, o
             slots = slice(s0, s0 + count)
             nc.vector.tensor_tensor(window[:].indirect(lists(s0, count)), y[h][:, slots], gates[:, slots], MULT)
 
-        def add_and_store(h, queue):
+        def add_and_store(h, window, queue):
             for t0, width in STORES:
                 cols = slice(t0, t0 + width)
-                nc.vector.tensor_tensor(total[h][:, cols], landing[h][:, cols], residual[h][:, cols], ADD)
+                nc.vector.tensor_tensor(total[h][:, cols], window[:, cols], residual[h][:, cols], ADD)
                 queue.dma_start(out[h * P : (h + 1) * P, cols], total[h][:, cols])
 
-        def add_by_transposes_and_store(h, queue):
-            banks = []
-            for t0 in range(0, T, BANK):
-                turned = turned_banks.tile([P, BANK], F32, name="turned")
-                for c0 in range(0, BANK, P):
-                    block = residual[h][:, t0 + c0 : t0 + c0 + P]
-                    nc.tensor.matmul(turned[:, c0 : c0 + P], block, identity[:], start=c0 == 0, stop=False, is_transpose=True)
-                banks.append(turned)
-            for t0, turned in zip(range(0, T, BANK), banks):
-                for c0 in range(0, BANK, P):
-                    block = first_landing[:, t0 + c0 : t0 + c0 + P]
-                    nc.tensor.matmul(turned[:, c0 : c0 + P], block, identity[:], start=False, stop=False, is_transpose=True)
+        def add_by_transposes_and_store(h, addends, queue):
+            banks = [turned_banks.tile([P, BANK], F32, name="turned") for t0 in range(0, T, BANK)]
             sums = []
-            for t0, turned in zip(range(0, T, BANK), banks):
-                for c0 in range(0, BANK, P):
-                    block = landing[h][:, t0 + c0 : t0 + c0 + P]
-                    nc.tensor.matmul(turned[:, c0 : c0 + P], block, identity[:], start=False, stop=c0 == BANK - P, is_transpose=True)
-                part = keep.tile([P, BANK], F32, name=f"sums{t0}", align_bytes=64)
-                nc.scalar.copy(part[:], turned[:])
-                sums.append(part)
+            for i, addend in enumerate(addends):
+                last = i == len(addends) - 1
+                for t0, turned in zip(range(0, T, BANK), banks):
+                    for c0 in range(0, BANK, P):
+                        nc.tensor.matmul(
+                            turned[:, c0 : c0 + P],
+                            addend[:, t0 + c0 : t0 + c0 + P],
+                            identity[:],
+                            start=i == 0 and c0 == 0,
+                            stop=last and c0 == BANK - P,
+                            is_transpose=True,
+                        )
+                    if last:
+                        part = keep.tile([P, BANK], F32, name=f"sums{t0}", align_bytes=64)
+                        nc.scalar.copy(part[:], turned[:])
+                        sums.append(part)
             for t0, part in zip(range(0, T, BANK), sums):
                 back = back_banks.tile([P, BANK], F32, name="back")
                 for c0 in range(0, BANK, P):
@@ -196,30 +178,30 @@ def tile_moe_res_lin_gelu_kernel(tc, xT, xr, w_words, w_scales, b, gate, offs, o
                 nc.scalar.copy(total[h][:, cols], back[:])
                 queue.dma_start(out[h * P : (h + 1) * P, cols], total[h][:, cols])
 
-        nc.vector.tensor_copy(row2[:], raw2[:])
-        nc.vector.tensor_copy(slot_row(0, VECTOR_SLOTS, 2), raw2[:].indirect(lists(0, VECTOR_SLOTS)))
-        gather_row(VECTOR_SLOTS, GROUP - VECTOR_SLOTS, 2, row2)
-        gather_row(GROUP, GROUP, 2, row2)
-        for raw, (t0, width) in zip(raw_pairs, PAIR_CHUNKS):
-            nc.vector.tensor_copy(pair_values[:, t0 : t0 + width, :], raw[:].rearrange("p j t -> p t j"))
-        nc.vector.tensor_copy(slot_pairs(0), pairs.indirect(lists(0, GROUP)))
-        nc.vector.tensor_copy(slot_row(0, VECTOR_SLOTS, 3), raw3.indirect(lists(0, VECTOR_SLOTS)))
-        nc.vector.tensor_copy(slot_pairs(1), pair_tile[:, 0 : T + SPARE].indirect(lists(GROUP, GROUP)))
-        cast_row(row3, raw3, LAST_ROW_CHUNKS)
-        gather_row(VECTOR_SLOTS, GROUP - VECTOR_SLOTS, 3, row3)
-        for s0 in range(GROUP, S, PIECE):
-            gather_row(s0, PIECE, 3, row3)
+        for j in range(PACK):
+            for cols in chunks(j):
+                if j == 0 and cols.start > 0:
+                    nc.scalar.copy(rounded[j][:, cols], raw[j][:, cols])
+                else:
+                    nc.gpsimd.tensor_copy(rounded[j][:, cols], raw[j][:, cols])
+            last = j == PACK - 1
+            for s0, s1 in pieces(0, PIECE if last else 0, VECTOR_SLOTS):
+                nc.vector.tensor_copy(slot_row(s0, s1 - s0, j), raw[j][:].indirect(lists(s0, s1 - s0)))
+            for s0, s1 in pieces(VECTOR_SLOTS, S - PIECE if last else S, S):
+                nc.scalar.activation(slot_row(s0, s1 - s0, j), rounded[j][:].indirect(lists(s0, s1 - s0)), COPY)
         for s0 in range(0, S, PIECE):
             quantise(s0, PIECE)
+        last_window = keep.tile([P, T], F32, name="last_window", tag="slots_then_window", align_bytes=64)
+        nc.gpsimd.memset(last_window[:], 0.0)
         experts(0, 0)
-        scatter(landing[0], 0, PAIR, 0)
+        scatter(windows[0], 0, PAIR, 0)
         experts(1, 0)
-        scatter(first_landing, PAIR, PAIR, 0)
+        scatter(windows[1], PAIR, PAIR, 0)
         for pair in range(2, E // 2):
             experts(pair, 0)
-        scatter(landing[0], GROUP, GROUP, 0)
+        scatter(windows[0], GROUP, GROUP, 0)
         for pair in range(E // 2):
             experts(pair, 1)
-        scatter(landing[1], 0, S, 1)
-        add_by_transposes_and_store(0, nc.scalar)
-        add_and_store(1, nc.sync)
+        scatter(last_window, 0, S, 1)
+        add_by_transposes_and_store(0, [residual[0], windows[1], windows[0]], nc.scalar)
+        add_and_store(1, last_window, nc.sync)

@@ -1,4 +1,5 @@
 from contextlib import ExitStack
+from itertools import accumulate
 
 import concourse.mybir as mybir
 from concourse.masks import make_identity
@@ -24,8 +25,9 @@ COPY = mybir.ActivationFunctionType.Copy
 FLOPS = 2 * K * N * S
 BYTES = 4 * K * T + 4 * N * T + E * K * N + E * (K // 32) * N + 4 * N * E + 4 * S + 2 * S + 4 * N * T
 
-ROW_LOADS = [2, 2, 2, 3]
-VECTOR_SLOTS = 576
+ROW_LOADS = [(768, 768), (1024, 512), (1024, 512), (768, 512, 256)]
+VECTOR_SLOTS = 320
+SCALAR_WEAVES = 128
 GROUP = 512
 PIECE = 256
 PAIR = 2 * C
@@ -55,7 +57,8 @@ def tile_moe_res_lin_gelu_kernel(tc, xT, xr, w_words, w_scales, b, gate, offs, o
         residual = [keep.tile([P, T], F32, name=f"residual{h}", align_bytes=64) for h in range(HALVES)]
         total = [keep.tile([P, T], F32, name=f"total{h}", align_bytes=64) for h in range(HALVES)]
         y = [keep.tile([P, S], F32, name=f"y{h}", align_bytes=64) for h in range(HALVES)]
-        grouped = keep.tile([P, S * PACK], BF16, name="grouped", tag="slots_then_window", align_bytes=64)
+        pairs = keep.tile([P, 2 * S], U32, name="pairs", align_bytes=64)
+        grouped = keep.tile([P, S * PACK], BF16, name="grouped", align_bytes=64)
         codes = [keep.tile([P, GROUP], U32, name=f"x_codes{g}", align_bytes=64) for g in range(S // GROUP)]
         scales = [keep.tile([P, GROUP], U8, name=f"x_scales{g}", align_bytes=64) for g in range(S // GROUP)]
 
@@ -66,13 +69,16 @@ def tile_moe_res_lin_gelu_kernel(tc, xT, xr, w_words, w_scales, b, gate, offs, o
         nc.vector.memset(warm[:], 0.0)
         nc.scalar.activation(warm_out[:], warm[:], GELU)
         for window in windows:
-            nc.vector.memset(window[:], 0.0)
+            nc.vector.memset(window[:].bitcast(I32), 0)
+
+        last_window = keep.tile([P, T], F32, name="last_window", align_bytes=64)
+        nc.gpsimd.memset(last_window[:], 0.0)
 
         rows = xT.rearrange("(p j) t -> p j t", j=PACK)
 
         def chunks(j):
-            width = T // ROW_LOADS[j]
-            return [slice(t0, t0 + width) for t0 in range(0, T, width)]
+            ends = list(accumulate(ROW_LOADS[j]))
+            return [slice(end - width, end) for width, end in zip(ROW_LOADS[j], ends)]
 
         for j in range(PACK):
             for cols in chunks(j):
@@ -109,10 +115,13 @@ def tile_moe_res_lin_gelu_kernel(tc, xT, xr, w_words, w_scales, b, gate, offs, o
             return offsets[:, s0 // 16 : (s0 + count) // 16]
 
         def slot_row(s0, count, j):
-            return grouped[:].rearrange("p (s j) -> p s j", j=PACK)[:, s0 : s0 + count, j]
+            first = (j // 2) * S + s0
+            return pairs[:, first : first + count].bitcast(BF16).rearrange("p (s i) -> p s i", i=2)[:, :, j % 2]
 
-        def pieces(s0, cut, s1):
-            return [(a, z) for a, z in ((s0, cut), (cut, s1)) if z > a]
+        def weave(s0, count):
+            copy, dtype = (nc.scalar.copy, U32) if s0 + count == S else (nc.vector.tensor_copy, I32)
+            words = grouped[:].bitcast(dtype)[:, 2 * s0 : 2 * (s0 + count)].rearrange("p (s u) -> p s u", u=2)
+            copy(words, pairs[:].bitcast(dtype).rearrange("p (u s) -> p s u", u=2)[:, s0 : s0 + count, :])
 
         def quantise(s0, count):
             g, c0 = divmod(s0, GROUP)
@@ -180,19 +189,18 @@ def tile_moe_res_lin_gelu_kernel(tc, xT, xr, w_words, w_scales, b, gate, offs, o
 
         for j in range(PACK):
             for cols in chunks(j):
-                if j == 0 and cols.start > 0:
-                    nc.scalar.copy(rounded[j][:, cols], raw[j][:, cols])
-                else:
-                    nc.gpsimd.tensor_copy(rounded[j][:, cols], raw[j][:, cols])
-            last = j == PACK - 1
-            for s0, s1 in pieces(0, PIECE if last else 0, VECTOR_SLOTS):
-                nc.vector.tensor_copy(slot_row(s0, s1 - s0, j), raw[j][:].indirect(lists(s0, s1 - s0)))
-            for s0, s1 in pieces(VECTOR_SLOTS, S - PIECE if last else S, S):
+                copy = nc.scalar.copy if j == 0 and cols.start == 0 else nc.vector.tensor_copy
+                copy(rounded[j][:, cols], raw[j][:, cols])
+            nc.vector.tensor_copy(slot_row(0, VECTOR_SLOTS, j), raw[j][:].indirect(lists(0, VECTOR_SLOTS)))
+            cuts = [VECTOR_SLOTS] + (list(range(GROUP, S, PIECE)) if j == PACK - 1 else []) + [S]
+            for s0, s1 in zip(cuts, cuts[1:]):
                 nc.scalar.activation(slot_row(s0, s1 - s0, j), rounded[j][:].indirect(lists(s0, s1 - s0)), COPY)
         for s0 in range(0, S, PIECE):
-            quantise(s0, PIECE)
-        last_window = keep.tile([P, T], F32, name="last_window", tag="slots_then_window", align_bytes=64)
-        nc.gpsimd.memset(last_window[:], 0.0)
+            weave(s0, min(PIECE, S - SCALAR_WEAVES - s0))
+            if s0 > 0:
+                quantise(s0 - PIECE, PIECE)
+        weave(S - SCALAR_WEAVES, SCALAR_WEAVES)
+        quantise(S - PIECE, PIECE)
         experts(0, 0)
         scatter(windows[0], 0, PAIR, 0)
         experts(1, 0)

@@ -28,6 +28,7 @@ BYTES = 4 * K * T + 4 * N * T + E * K * N + E * (K // 32) * N + 4 * N * E + 4 * 
 ROW_LOADS = [(768, 768), (1024, 512), (1024, 512), (768, 512, 256)]
 VECTOR_SLOTS = 320
 SCALAR_WEAVES = 128
+SCALAR_ROUNDS = 1024
 GROUP = 512
 PIECE = 256
 PAIR = 2 * C
@@ -58,7 +59,7 @@ def tile_moe_res_lin_gelu_kernel(tc, xT, xr, w_words, w_scales, b, gate, offs, o
         total = [keep.tile([P, T], F32, name=f"total{h}", align_bytes=64) for h in range(HALVES)]
         y = [keep.tile([P, S], F32, name=f"y{h}", align_bytes=64) for h in range(HALVES)]
         pairs = keep.tile([P, 2 * S], U32, name="pairs", align_bytes=64)
-        grouped = keep.tile([P, S * PACK], BF16, name="grouped", align_bytes=64)
+        grouped = keep.tile([P, S * PACK], BF16, name="grouped", tag="slots_then_window", align_bytes=64)
         codes = [keep.tile([P, GROUP], U32, name=f"x_codes{g}", align_bytes=64) for g in range(S // GROUP)]
         scales = [keep.tile([P, GROUP], U8, name=f"x_scales{g}", align_bytes=64) for g in range(S // GROUP)]
 
@@ -71,9 +72,6 @@ def tile_moe_res_lin_gelu_kernel(tc, xT, xr, w_words, w_scales, b, gate, offs, o
         for window in windows:
             nc.vector.memset(window[:].bitcast(I32), 0)
 
-        last_window = keep.tile([P, T], F32, name="last_window", align_bytes=64)
-        nc.gpsimd.memset(last_window[:], 0.0)
-
         rows = xT.rearrange("(p j) t -> p j t", j=PACK)
 
         def chunks(j):
@@ -83,8 +81,8 @@ def tile_moe_res_lin_gelu_kernel(tc, xT, xr, w_words, w_scales, b, gate, offs, o
         for j in range(PACK):
             for cols in chunks(j):
                 nc.sync.dma_start(raw[j][:, cols], rows[:, j, cols])
-                if j == 0 and cols.start == 0:
-                    nc.sync.dma_start(offsets[:], offs)
+            if j == 0:
+                nc.sync.dma_start(offsets[:], offs)
 
         def load_scales(g):
             for q in range(4):
@@ -99,11 +97,11 @@ def tile_moe_res_lin_gelu_kernel(tc, xT, xr, w_words, w_scales, b, gate, offs, o
                 w_words[2 * i : 2 * i + 2, 0].rearrange("e p n r -> p e (n r)").bitcast(I32),
             )
 
-        load_scales(0)
         load_weights(0)
+        load_scales(0)
         nc.sync.dma_start(bias[:], b.rearrange("(h p) e -> p h e", p=P))
-        load_weights(1)
         nc.sync.dma_start(gates[:, 0:GROUP], gate[0:P, 0:GROUP])
+        load_weights(1)
         load_scales(1)
         load_weights(2)
         load_weights(3)
@@ -131,23 +129,23 @@ def tile_moe_res_lin_gelu_kernel(tc, xT, xr, w_words, w_scales, b, gate, offs, o
                 in_=grouped[:, s0 * PACK : (s0 + count) * PACK],
             )
 
-        def experts(pair, h):
+        def experts(first, count, h):
             acc = psum.tile([P, PAIR], F32, name="acc")
-            for k in range(2):
-                e = 2 * pair + k
+            for k in range(count):
+                e = first + k
                 i, c0 = divmod(e * C, GROUP)
-                col = k * N + h * P
+                col = (e % 2) * N + h * P
                 nc.tensor.matmul_mx(
                     out=acc[:, k * C : (k + 1) * C],
-                    lhsT=w_codes[pair][:, col * PACK : (col + P) * PACK].bitcast(FP8X4),
+                    lhsT=w_codes[e // 2][:, col * PACK : (col + P) * PACK].bitcast(FP8X4),
                     lhsT_scale=w_planes[e // PLANES][4 * (e % PLANES) : P, h * P : (h + 1) * P],
                     rhs=codes[i][:, c0 : c0 + C].bitcast(FP8X4),
                     rhs_scale=scales[i][:, c0 : c0 + C],
                     start=True,
                     stop=True,
                 )
-            for k in range(2):
-                e = 2 * pair + k
+            for k in range(count):
+                e = first + k
                 nc.scalar.activation(y[h][:, e * C : (e + 1) * C], acc[:, k * C : (k + 1) * C], GELU, bias=bias[:, h, e : e + 1])
 
         def scatter(window, s0, count, h):
@@ -189,27 +187,35 @@ def tile_moe_res_lin_gelu_kernel(tc, xT, xr, w_words, w_scales, b, gate, offs, o
 
         for j in range(PACK):
             for cols in chunks(j):
-                copy = nc.scalar.copy if j == 0 and cols.start == 0 else nc.vector.tensor_copy
-                copy(rounded[j][:, cols], raw[j][:, cols])
+                cut = cols.start if j > 0 else min(cols.stop, SCALAR_ROUNDS)
+                if cut > cols.start:
+                    nc.scalar.copy(rounded[j][:, cols.start : cut], raw[j][:, cols.start : cut])
+                if cut < cols.stop:
+                    nc.vector.tensor_copy(rounded[j][:, cut : cols.stop], raw[j][:, cut : cols.stop])
             nc.vector.tensor_copy(slot_row(0, VECTOR_SLOTS, j), raw[j][:].indirect(lists(0, VECTOR_SLOTS)))
             cuts = [VECTOR_SLOTS] + (list(range(GROUP, S, PIECE)) if j == PACK - 1 else []) + [S]
             for s0, s1 in zip(cuts, cuts[1:]):
                 nc.scalar.activation(slot_row(s0, s1 - s0, j), rounded[j][:].indirect(lists(s0, s1 - s0)), COPY)
-        for s0 in range(0, S, PIECE):
-            weave(s0, min(PIECE, S - SCALAR_WEAVES - s0))
-            if s0 > 0:
-                quantise(s0 - PIECE, PIECE)
+        cuts = [0, C] + list(range(PIECE, S, PIECE)) + [S]
+        steps = list(zip(cuts, cuts[1:]))
+        for i, (s0, s1) in enumerate(steps):
+            weave(s0, min(s1, S - SCALAR_WEAVES) - s0)
+            if i > 0:
+                quantise(steps[i - 1][0], s0 - steps[i - 1][0])
         weave(S - SCALAR_WEAVES, SCALAR_WEAVES)
         quantise(S - PIECE, PIECE)
-        experts(0, 0)
+        last_window = keep.tile([P, T], F32, name="last_window", tag="slots_then_window", align_bytes=64)
+        nc.gpsimd.memset(last_window[:], 0.0)
+        experts(0, 1, 0)
+        experts(1, 1, 0)
         scatter(windows[0], 0, PAIR, 0)
-        experts(1, 0)
+        experts(2, 2, 0)
         scatter(windows[1], PAIR, PAIR, 0)
-        for pair in range(2, E // 2):
-            experts(pair, 0)
+        for first in range(4, E, 2):
+            experts(first, 2, 0)
         scatter(windows[0], GROUP, GROUP, 0)
-        for pair in range(E // 2):
-            experts(pair, 1)
+        for first in range(0, E, 2):
+            experts(first, 2, 1)
         scatter(last_window, 0, S, 1)
         add_by_transposes_and_store(0, [residual[0], windows[1], windows[0]], nc.scalar)
         add_and_store(1, last_window, nc.sync)

@@ -2,7 +2,6 @@ from contextlib import ExitStack
 from itertools import accumulate
 
 import concourse.mybir as mybir
-from concourse.masks import make_identity
 
 K, T, E, C, N = 512, 1536, 8, 128, 256
 P = 128
@@ -32,8 +31,8 @@ SCALAR_ROUNDS = 1024
 GROUP = 512
 PIECE = 256
 PAIR = 2 * C
-BANK = 512
 PLANES = 4
+SCALAR_SCATTERS = [(0, 384), (384, 320), (704, 320)]
 STORES = [(0, 256), (256, 512), (768, 512), (1280, 256)]
 
 
@@ -41,9 +40,7 @@ def tile_moe_res_lin_gelu_kernel(tc, xT, xr, w_words, w_scales, b, gate, offs, o
     nc = tc.nc
     with ExitStack() as ctx:
         keep = ctx.enter_context(tc.tile_pool(name="keep", bufs=1))
-        psum = ctx.enter_context(tc.psum_pool(name="psum", bufs=3))
-        turned_banks = ctx.enter_context(tc.psum_pool(name="turned_banks", bufs=3))
-        back_banks = ctx.enter_context(tc.psum_pool(name="back_banks", bufs=2))
+        psum = ctx.enter_context(tc.psum_pool(name="psum", bufs=8))
 
         offsets = keep.tile([P, S // 16], U16, name="offsets")
         w_codes = [keep.tile([P, 2 * N * PACK], U8, name=f"w_codes{i}", align_bytes=64) for i in range(E // 2)]
@@ -59,12 +56,11 @@ def tile_moe_res_lin_gelu_kernel(tc, xT, xr, w_words, w_scales, b, gate, offs, o
         total = [keep.tile([P, T], F32, name=f"total{h}", align_bytes=64) for h in range(HALVES)]
         y = [keep.tile([P, S], F32, name=f"y{h}", align_bytes=64) for h in range(HALVES)]
         pairs = keep.tile([P, 2 * S], U32, name="pairs", align_bytes=64)
-        grouped = keep.tile([P, S * PACK], BF16, name="grouped", tag="slots_then_window", align_bytes=64)
+        grouped = keep.tile([P, S * PACK], BF16, name="grouped", align_bytes=64)
         codes = [keep.tile([P, GROUP], U32, name=f"x_codes{g}", align_bytes=64) for g in range(S // GROUP)]
         scales = [keep.tile([P, GROUP], U8, name=f"x_scales{g}", align_bytes=64) for g in range(S // GROUP)]
 
-        identity = keep.tile([P, P], F32, name="identity", align_bytes=64)
-        make_identity(nc, identity[:])
+        gated = keep.tile([P, S], F32, name="gated", align_bytes=64)
         for planes in w_planes:
             nc.vector.memset(planes[:].bitcast(I32), 0)
         nc.vector.memset(warm[:], 0.0)
@@ -105,8 +101,8 @@ def tile_moe_res_lin_gelu_kernel(tc, xT, xr, w_words, w_scales, b, gate, offs, o
         load_scales(1)
         load_weights(2)
         load_weights(3)
-        nc.sync.dma_start(residual[0][:], xr[0:P, :])
         nc.sync.dma_start(gates[:, GROUP:S], gate[0:P, GROUP:S])
+        nc.sync.dma_start(residual[0][:], xr[0:P, :])
         nc.sync.dma_start(residual[1][:], xr[P:N, :])
 
         def lists(s0, count):
@@ -158,33 +154,6 @@ def tile_moe_res_lin_gelu_kernel(tc, xT, xr, w_words, w_scales, b, gate, offs, o
                 nc.vector.tensor_tensor(total[h][:, cols], window[:, cols], residual[h][:, cols], ADD)
                 queue.dma_start(out[h * P : (h + 1) * P, cols], total[h][:, cols])
 
-        def add_by_transposes_and_store(h, addends, queue):
-            banks = [turned_banks.tile([P, BANK], F32, name="turned") for t0 in range(0, T, BANK)]
-            sums = []
-            for i, addend in enumerate(addends):
-                last = i == len(addends) - 1
-                for t0, turned in zip(range(0, T, BANK), banks):
-                    for c0 in range(0, BANK, P):
-                        nc.tensor.matmul(
-                            turned[:, c0 : c0 + P],
-                            addend[:, t0 + c0 : t0 + c0 + P],
-                            identity[:],
-                            start=i == 0 and c0 == 0,
-                            stop=last and c0 == BANK - P,
-                            is_transpose=True,
-                        )
-                    if last:
-                        part = keep.tile([P, BANK], F32, name=f"sums{t0}", align_bytes=64)
-                        nc.scalar.copy(part[:], turned[:])
-                        sums.append(part)
-            for t0, part in zip(range(0, T, BANK), sums):
-                back = back_banks.tile([P, BANK], F32, name="back")
-                for c0 in range(0, BANK, P):
-                    nc.tensor.transpose(back[:, c0 : c0 + P], part[:, c0 : c0 + P], identity[:])
-                cols = slice(t0, t0 + BANK)
-                nc.scalar.copy(total[h][:, cols], back[:])
-                queue.dma_start(out[h * P : (h + 1) * P, cols], total[h][:, cols])
-
         for j in range(PACK):
             for cols in chunks(j):
                 cut = cols.start if j > 0 else min(cols.stop, SCALAR_ROUNDS)
@@ -204,18 +173,16 @@ def tile_moe_res_lin_gelu_kernel(tc, xT, xr, w_words, w_scales, b, gate, offs, o
                 quantise(steps[i - 1][0], s0 - steps[i - 1][0])
         weave(S - SCALAR_WEAVES, SCALAR_WEAVES)
         quantise(S - PIECE, PIECE)
-        last_window = keep.tile([P, T], F32, name="last_window", tag="slots_then_window", align_bytes=64)
-        nc.gpsimd.memset(last_window[:], 0.0)
         experts(0, 1, 0)
         experts(1, 1, 0)
+        for first, h in [(0, 1), (2, 1), (2, 0), (4, 1), (6, 1), (4, 0), (6, 0)]:
+            experts(first, 2, h)
         scatter(windows[0], 0, PAIR, 0)
-        experts(2, 2, 0)
-        scatter(windows[1], PAIR, PAIR, 0)
-        for first in range(4, E, 2):
-            experts(first, 2, 0)
+        nc.vector.tensor_tensor(gated[:, 0:GROUP], y[1][:, 0:GROUP], gates[:, 0:GROUP], MULT)
+        scatter(windows[0], PAIR, PAIR, 0)
+        nc.vector.tensor_tensor(gated[:, GROUP:S], y[1][:, GROUP:S], gates[:, GROUP:S], MULT)
         scatter(windows[0], GROUP, GROUP, 0)
-        for first in range(0, E, 2):
-            experts(first, 2, 1)
-        scatter(last_window, 0, S, 1)
-        add_by_transposes_and_store(0, [residual[0], windows[1], windows[0]], nc.scalar)
-        add_and_store(1, last_window, nc.sync)
+        for s0, count in SCALAR_SCATTERS:
+            nc.scalar.activation(windows[1][:].indirect(lists(s0, count)), gated[:, s0 : s0 + count], COPY)
+        for h in range(HALVES):
+            add_and_store(h, windows[h], nc.sync)

@@ -32,7 +32,7 @@ GROUP = 512
 PIECE = 256
 PAIR = 2 * C
 PLANES = 4
-SCALAR_SCATTERS = [(0, 384), (384, 320), (704, 320)]
+FIRST_GATED = 384
 STORES = [(0, 256), (256, 512), (768, 512), (1280, 256)]
 
 
@@ -43,7 +43,7 @@ def tile_moe_res_lin_gelu_kernel(tc, xT, xr, w_words, w_scales, b, gate, offs, o
         psum = ctx.enter_context(tc.psum_pool(name="psum", bufs=8))
 
         offsets = keep.tile([P, S // 16], U16, name="offsets")
-        w_codes = [keep.tile([P, 2 * N * PACK], U8, name=f"w_codes{i}", align_bytes=64) for i in range(E // 2)]
+        w_codes = [keep.tile([P, 2 * N * PACK], U8, name=f"w_codes{i}", tag=f"w_codes{i}", align_bytes=64) for i in range(E // 2)]
         w_planes = [keep.tile([P, N], U8, name=f"w_planes{g}", align_bytes=64) for g in range(E // PLANES)]
         bias = keep.tile([P, HALVES, E], F32, name="bias")
         gates = keep.tile([P, S], F32, name="gates")
@@ -60,7 +60,6 @@ def tile_moe_res_lin_gelu_kernel(tc, xT, xr, w_words, w_scales, b, gate, offs, o
         codes = [keep.tile([P, GROUP], U32, name=f"x_codes{g}", align_bytes=64) for g in range(S // GROUP)]
         scales = [keep.tile([P, GROUP], U8, name=f"x_scales{g}", align_bytes=64) for g in range(S // GROUP)]
 
-        gated = keep.tile([P, S], F32, name="gated", align_bytes=64)
         for planes in w_planes:
             nc.vector.memset(planes[:].bitcast(I32), 0)
         nc.vector.memset(warm[:], 0.0)
@@ -175,14 +174,19 @@ def tile_moe_res_lin_gelu_kernel(tc, xT, xr, w_words, w_scales, b, gate, offs, o
         quantise(S - PIECE, PIECE)
         experts(0, 1, 0)
         experts(1, 1, 0)
-        for first, h in [(0, 1), (2, 1), (2, 0), (4, 1), (6, 1), (4, 0), (6, 0)]:
+        for first, h in [(0, 1), (2, 1), (2, 0), (4, 1), (4, 0), (6, 1), (6, 0)]:
             experts(first, 2, h)
         scatter(windows[0], 0, PAIR, 0)
-        nc.vector.tensor_tensor(gated[:, 0:GROUP], y[1][:, 0:GROUP], gates[:, 0:GROUP], MULT)
-        scatter(windows[0], PAIR, PAIR, 0)
-        nc.vector.tensor_tensor(gated[:, GROUP:S], y[1][:, GROUP:S], gates[:, GROUP:S], MULT)
-        scatter(windows[0], GROUP, GROUP, 0)
-        for s0, count in SCALAR_SCATTERS:
-            nc.scalar.activation(windows[1][:].indirect(lists(s0, count)), gated[:, s0 : s0 + count], COPY)
+        gated = [
+            keep.tile([P, FIRST_GATED], F32, name="gated0", tag=f"w_codes{E // 2 - 1}", align_bytes=64),
+            keep.tile([P, S - FIRST_GATED], F32, name="gated1", align_bytes=64),
+        ]
+        nc.vector.tensor_tensor(gated[0][:], y[1][:, 0:FIRST_GATED], gates[:, 0:FIRST_GATED], MULT)
+        nc.vector.tensor_tensor(gated[1][:], y[1][:, FIRST_GATED:S], gates[:, FIRST_GATED:S], MULT)
+        scatter(windows[0], PAIR, S - PAIR, 0)
+        rest = (S - FIRST_GATED) // 2
+        nc.scalar.activation(windows[1][:].indirect(lists(0, FIRST_GATED)), gated[0][:], COPY)
+        for c0 in (0, rest):
+            nc.scalar.activation(windows[1][:].indirect(lists(FIRST_GATED + c0, rest)), gated[1][:, c0 : c0 + rest], COPY)
         for h in range(HALVES):
             add_and_store(h, windows[h], nc.sync)

@@ -1,5 +1,4 @@
 from contextlib import ExitStack
-from itertools import accumulate
 
 import concourse.mybir as mybir
 
@@ -24,15 +23,13 @@ COPY = mybir.ActivationFunctionType.Copy
 FLOPS = 2 * K * N * S
 BYTES = 4 * K * T + 4 * N * T + E * K * N + E * (K // 32) * N + 4 * N * E + 4 * S + 2 * S + 4 * N * T
 
-ROW_LOADS = [(768, 768), (1024, 512), (1024, 512), (768, 512, 256)]
-VECTOR_SLOTS = 320
-SCALAR_WEAVES = 128
-SCALAR_ROUNDS = 1024
+VECTOR_SLOTS = 448
+SCALAR_SLOTS = S - VECTOR_SLOTS
 GROUP = 512
 PIECE = 256
 PAIR = 2 * C
 PLANES = 4
-FIRST_GATED = 384
+FIRST_GATED = 256
 STORES = [(0, 256), (256, 512), (768, 512), (1280, 256)]
 
 
@@ -48,14 +45,14 @@ def tile_moe_res_lin_gelu_kernel(tc, xT, xr, w_words, w_scales, b, gate, offs, o
         bias = keep.tile([P, HALVES, E], F32, name="bias")
         gates = keep.tile([P, S], F32, name="gates")
         raw = [keep.tile([P, T], F32, name=f"raw{j}", align_bytes=64) for j in range(PACK)]
-        rounded = [keep.tile([P, T], BF16, name=f"rounded{j}", align_bytes=64) for j in range(PACK)]
         warm = keep.tile([P, 1], F32, name="warm")
         warm_out = keep.tile([P, 1], F32, name="warm_out")
         windows = [keep.tile([P, T], F32, name=f"window{i}", align_bytes=64) for i in range(2)]
         residual = [keep.tile([P, T], F32, name=f"residual{h}", align_bytes=64) for h in range(HALVES)]
         total = [keep.tile([P, T], F32, name=f"total{h}", align_bytes=64) for h in range(HALVES)]
         y = [keep.tile([P, S], F32, name=f"y{h}", align_bytes=64) for h in range(HALVES)]
-        pairs = keep.tile([P, 2 * S], U32, name="pairs", align_bytes=64)
+        pairs = keep.tile([P, 2 * VECTOR_SLOTS], U32, name="pairs", align_bytes=64)
+        singles = [keep.tile([P, 2 * SCALAR_SLOTS], BF16, name=f"singles{u}", align_bytes=64) for u in range(2)]
         grouped = keep.tile([P, S * PACK], BF16, name="grouped", align_bytes=64)
         codes = [keep.tile([P, GROUP], U32, name=f"x_codes{g}", align_bytes=64) for g in range(S // GROUP)]
         scales = [keep.tile([P, GROUP], U8, name=f"x_scales{g}", align_bytes=64) for g in range(S // GROUP)]
@@ -69,13 +66,8 @@ def tile_moe_res_lin_gelu_kernel(tc, xT, xr, w_words, w_scales, b, gate, offs, o
 
         rows = xT.rearrange("(p j) t -> p j t", j=PACK)
 
-        def chunks(j):
-            ends = list(accumulate(ROW_LOADS[j]))
-            return [slice(end - width, end) for width, end in zip(ROW_LOADS[j], ends)]
-
         for j in range(PACK):
-            for cols in chunks(j):
-                nc.sync.dma_start(raw[j][:, cols], rows[:, j, cols])
+            nc.sync.dma_start(raw[j][:], rows[:, j, :])
             if j == 0:
                 nc.sync.dma_start(offsets[:], offs)
 
@@ -95,26 +87,34 @@ def tile_moe_res_lin_gelu_kernel(tc, xT, xr, w_words, w_scales, b, gate, offs, o
         load_weights(0)
         load_scales(0)
         nc.sync.dma_start(bias[:], b.rearrange("(h p) e -> p h e", p=P))
-        nc.sync.dma_start(gates[:, 0:GROUP], gate[0:P, 0:GROUP])
+        nc.sync.dma_start(gates[:, 0:PAIR], gate[0:P, 0:PAIR])
         load_weights(1)
         load_scales(1)
         load_weights(2)
         load_weights(3)
-        nc.sync.dma_start(gates[:, GROUP:S], gate[0:P, GROUP:S])
+        nc.sync.dma_start(gates[:, PAIR:S], gate[0:P, PAIR:S])
         nc.sync.dma_start(residual[0][:], xr[0:P, :])
         nc.sync.dma_start(residual[1][:], xr[P:N, :])
 
         def lists(s0, count):
             return offsets[:, s0 // 16 : (s0 + count) // 16]
 
-        def slot_row(s0, count, j):
-            first = (j // 2) * S + s0
+        def pair_row(s0, count, j):
+            first = (j // 2) * VECTOR_SLOTS + s0
             return pairs[:, first : first + count].bitcast(BF16).rearrange("p (s i) -> p s i", i=2)[:, :, j % 2]
 
-        def weave(s0, count):
-            copy, dtype = (nc.scalar.copy, U32) if s0 + count == S else (nc.vector.tensor_copy, I32)
-            words = grouped[:].bitcast(dtype)[:, 2 * s0 : 2 * (s0 + count)].rearrange("p (s u) -> p s u", u=2)
-            copy(words, pairs[:].bitcast(dtype).rearrange("p (u s) -> p s u", u=2)[:, s0 : s0 + count, :])
+        def single_row(s0, count, j):
+            first = (j % 2) * SCALAR_SLOTS + s0 - VECTOR_SLOTS
+            return singles[j // 2][:, first : first + count]
+
+        def weave_pairs(s0, count):
+            words = grouped[:].bitcast(I32)[:, 2 * s0 : 2 * (s0 + count)].rearrange("p (s u) -> p s u", u=2)
+            nc.vector.tensor_copy(words, pairs[:].bitcast(I32).rearrange("p (u s) -> p s u", u=2)[:, s0 : s0 + count, :])
+
+        def weave_singles(copy, s0, count, u):
+            c0 = s0 - VECTOR_SLOTS
+            slots = grouped[:, s0 * PACK : (s0 + count) * PACK].rearrange("p (s j) -> p s j", j=PACK)
+            copy(slots[:, :, 2 * u : 2 * u + 2], singles[u][:].rearrange("p (i s) -> p s i", i=2)[:, c0 : c0 + count, :])
 
         def quantise(s0, count):
             g, c0 = divmod(s0, GROUP)
@@ -154,27 +154,25 @@ def tile_moe_res_lin_gelu_kernel(tc, xT, xr, w_words, w_scales, b, gate, offs, o
                 queue.dma_start(out[h * P : (h + 1) * P, cols], total[h][:, cols])
 
         for j in range(PACK):
-            for cols in chunks(j):
-                cut = cols.start if j > 0 else min(cols.stop, SCALAR_ROUNDS)
-                if cut > cols.start:
-                    nc.scalar.copy(rounded[j][:, cols.start : cut], raw[j][:, cols.start : cut])
-                if cut < cols.stop:
-                    nc.vector.tensor_copy(rounded[j][:, cut : cols.stop], raw[j][:, cut : cols.stop])
-            nc.vector.tensor_copy(slot_row(0, VECTOR_SLOTS, j), raw[j][:].indirect(lists(0, VECTOR_SLOTS)))
-            cuts = [VECTOR_SLOTS] + (list(range(GROUP, S, PIECE)) if j == PACK - 1 else []) + [S]
+            last = j == PACK - 1
+            cuts = [0, PIECE, VECTOR_SLOTS] if last else [0, VECTOR_SLOTS]
             for s0, s1 in zip(cuts, cuts[1:]):
-                nc.scalar.activation(slot_row(s0, s1 - s0, j), rounded[j][:].indirect(lists(s0, s1 - s0)), COPY)
-        cuts = [0, C] + list(range(PIECE, S, PIECE)) + [S]
-        steps = list(zip(cuts, cuts[1:]))
-        for i, (s0, s1) in enumerate(steps):
-            weave(s0, min(s1, S - SCALAR_WEAVES) - s0)
-            if i > 0:
-                quantise(steps[i - 1][0], s0 - steps[i - 1][0])
-        weave(S - SCALAR_WEAVES, SCALAR_WEAVES)
-        quantise(S - PIECE, PIECE)
-        experts(0, 1, 0)
-        experts(1, 1, 0)
-        for first, h in [(0, 1), (2, 1), (2, 0), (4, 1), (4, 0), (6, 1), (6, 0)]:
+                nc.vector.tensor_copy(pair_row(s0, s1 - s0, j), raw[j][:].indirect(lists(s0, s1 - s0)))
+            cuts = [VECTOR_SLOTS, S - PIECE, S] if j % 2 else [VECTOR_SLOTS, S]
+            for s0, s1 in zip(cuts, cuts[1:]):
+                nc.scalar.activation(single_row(s0, s1 - s0, j), raw[j][:].indirect(lists(s0, s1 - s0)), COPY)
+            if j == 1:
+                for s0, s1 in zip(cuts, cuts[1:]):
+                    weave_singles(nc.vector.tensor_copy, s0, s1 - s0, 0)
+        weave_pairs(0, PIECE)
+        weave_pairs(PIECE, VECTOR_SLOTS - PIECE)
+        quantise(0, PIECE)
+        weave_singles(nc.vector.tensor_copy, VECTOR_SLOTS, GROUP - VECTOR_SLOTS, 1)
+        weave_singles(nc.vector.tensor_copy, GROUP, PIECE, 1)
+        weave_singles(nc.scalar.copy, S - PIECE, PIECE, 1)
+        for s0 in range(PIECE, S, PIECE):
+            quantise(s0, PIECE)
+        for first, h in [(0, 0), (0, 1), (2, 1), (2, 0), (4, 1), (4, 0), (6, 1), (6, 0)]:
             experts(first, 2, h)
         scatter(windows[0], 0, PAIR, 0)
         gated = [
@@ -189,4 +187,4 @@ def tile_moe_res_lin_gelu_kernel(tc, xT, xr, w_words, w_scales, b, gate, offs, o
         for c0 in (0, rest):
             nc.scalar.activation(windows[1][:].indirect(lists(FIRST_GATED + c0, rest)), gated[1][:, c0 : c0 + rest], COPY)
         for h in range(HALVES):
-            add_and_store(h, windows[h], nc.sync)
+            add_and_store(h, windows[h], (nc.sync, nc.scalar)[h])

@@ -23,13 +23,11 @@ COPY = mybir.ActivationFunctionType.Copy
 FLOPS = 2 * K * N * S
 BYTES = 4 * K * T + 4 * N * T + E * K * N + E * (K // 32) * N + 4 * N * E + 4 * S + 2 * S + 4 * N * T
 
-VECTOR_SLOTS = 448
-SCALAR_SLOTS = S - VECTOR_SLOTS
-GROUP = 512
-PIECE = 256
-PAIR = 2 * C
-PLANES = 4
-FIRST_GATED = 256
+GROUP = 2 * C
+GROUPS = S // GROUP
+PLAIN = S - GROUP
+HELP = 128
+SCALAR_SCATTER = 384
 STORES = [(0, 256), (256, 512), (768, 512), (1280, 256)]
 
 
@@ -40,8 +38,8 @@ def tile_moe_res_lin_gelu_kernel(tc, xT, xr, w_words, w_scales, b, gate, offs, o
         psum = ctx.enter_context(tc.psum_pool(name="psum", bufs=8))
 
         offsets = keep.tile([P, S // 16], U16, name="offsets")
-        w_codes = [keep.tile([P, 2 * N * PACK], U8, name=f"w_codes{i}", tag=f"w_codes{i}", align_bytes=64) for i in range(E // 2)]
-        w_planes = [keep.tile([P, N], U8, name=f"w_planes{g}", align_bytes=64) for g in range(E // PLANES)]
+        w_codes = [keep.tile([P, 4 * N * PACK], U8, name=f"w_codes{i}", align_bytes=64) for i in range(2)]
+        w_planes = keep.tile([P, E * N], U8, name="w_planes", align_bytes=64)
         bias = keep.tile([P, HALVES, E], F32, name="bias")
         gates = keep.tile([P, S], F32, name="gates")
         raw = [keep.tile([P, T], F32, name=f"raw{j}", align_bytes=64) for j in range(PACK)]
@@ -51,14 +49,13 @@ def tile_moe_res_lin_gelu_kernel(tc, xT, xr, w_words, w_scales, b, gate, offs, o
         residual = [keep.tile([P, T], F32, name=f"residual{h}", align_bytes=64) for h in range(HALVES)]
         total = [keep.tile([P, T], F32, name=f"total{h}", align_bytes=64) for h in range(HALVES)]
         y = [keep.tile([P, S], F32, name=f"y{h}", align_bytes=64) for h in range(HALVES)]
-        pairs = keep.tile([P, 2 * VECTOR_SLOTS], U32, name="pairs", align_bytes=64)
-        singles = [keep.tile([P, 2 * SCALAR_SLOTS], BF16, name=f"singles{u}", align_bytes=64) for u in range(2)]
-        grouped = keep.tile([P, S * PACK], BF16, name="grouped", align_bytes=64)
-        codes = [keep.tile([P, GROUP], U32, name=f"x_codes{g}", align_bytes=64) for g in range(S // GROUP)]
-        scales = [keep.tile([P, GROUP], U8, name=f"x_scales{g}", align_bytes=64) for g in range(S // GROUP)]
+        gated = keep.tile([P, S], F32, name="gated", align_bytes=64)
+        singles = [keep.tile([P, 2 * PLAIN], BF16, name=f"singles{u}", align_bytes=64) for u in range(2)]
+        grouped = [keep.tile([P, GROUP * PACK], BF16, name=f"grouped{g}", align_bytes=64) for g in range(GROUPS)]
+        codes = [keep.tile([P, GROUP], U32, name=f"x_codes{g}", align_bytes=64) for g in range(GROUPS)]
+        scales = [keep.tile([P, GROUP], U8, name=f"x_scales{g}", align_bytes=64) for g in range(GROUPS)]
 
-        for planes in w_planes:
-            nc.vector.memset(planes[:].bitcast(I32), 0)
+        nc.vector.memset(w_planes[:].bitcast(I32), 0)
         nc.vector.memset(warm[:], 0.0)
         nc.scalar.activation(warm_out[:], warm[:], GELU)
         for window in windows:
@@ -71,120 +68,104 @@ def tile_moe_res_lin_gelu_kernel(tc, xT, xr, w_words, w_scales, b, gate, offs, o
             if j == 0:
                 nc.sync.dma_start(offsets[:], offs)
 
-        def load_scales(g):
-            for q in range(4):
-                nc.sync.dma_start(
-                    w_planes[g][32 * q : 32 * q + 4 * PLANES, :].bitcast(I32),
-                    w_scales[PLANES * g : PLANES * (g + 1), 0, 4 * q : 4 * q + 4, :].bitcast(I32),
-                )
-
         def load_weights(i):
             nc.sync.dma_start(
-                w_codes[i][:].bitcast(I32).rearrange("p (e n) -> p e n", e=2),
-                w_words[2 * i : 2 * i + 2, 0].rearrange("e p n r -> p e (n r)").bitcast(I32),
+                w_codes[i][:].bitcast(I32).rearrange("p (e n) -> p e n", e=4),
+                w_words[4 * i : 4 * i + 4, 0].rearrange("e p n r -> p e (n r)").bitcast(I32),
             )
 
         load_weights(0)
-        load_scales(0)
+        for q in range(4):
+            nc.sync.dma_start(
+                w_planes[32 * q : 32 * q + 4, :].bitcast(I32).rearrange("r (e n) -> r e n", e=E),
+                w_scales[:, 0, 4 * q : 4 * q + 4, :].rearrange("e r n -> r e n").bitcast(I32),
+            )
         nc.sync.dma_start(bias[:], b.rearrange("(h p) e -> p h e", p=P))
-        nc.sync.dma_start(gates[:, 0:PAIR], gate[0:P, 0:PAIR])
         load_weights(1)
-        load_scales(1)
-        load_weights(2)
-        load_weights(3)
-        nc.sync.dma_start(gates[:, PAIR:S], gate[0:P, PAIR:S])
+        nc.sync.dma_start(gates[:, 0:GROUP], gate[0:P, 0:GROUP])
+        nc.sync.dma_start(gates[:, GROUP:S], gate[0:P, GROUP:S])
         nc.sync.dma_start(residual[0][:], xr[0:P, :])
         nc.sync.dma_start(residual[1][:], xr[P:N, :])
 
-        def lists(s0, count):
-            return offsets[:, s0 // 16 : (s0 + count) // 16]
+        def lists(s0, s1):
+            return offsets[:, s0 // 16 : s1 // 16]
 
-        def pair_row(s0, count, j):
-            first = (j // 2) * VECTOR_SLOTS + s0
-            return pairs[:, first : first + count].bitcast(BF16).rearrange("p (s i) -> p s i", i=2)[:, :, j % 2]
+        def slots_of(g):
+            return grouped[g][:].rearrange("p (s j) -> p s j", j=PACK)
 
-        def single_row(s0, count, j):
-            first = (j % 2) * SCALAR_SLOTS + s0 - VECTOR_SLOTS
-            return singles[j // 2][:, first : first + count]
+        def single_row(s0, s1, j):
+            first = (j % 2) * PLAIN - GROUP
+            return singles[j // 2][:, first + s0 : first + s1]
 
-        def weave_pairs(s0, count):
-            words = grouped[:].bitcast(I32)[:, 2 * s0 : 2 * (s0 + count)].rearrange("p (s u) -> p s u", u=2)
-            nc.vector.tensor_copy(words, pairs[:].bitcast(I32).rearrange("p (u s) -> p s u", u=2)[:, s0 : s0 + count, :])
+        def weave(copy, g, u):
+            c0 = (g - 1) * GROUP
+            copy(slots_of(g)[:, :, 2 * u : 2 * u + 2], singles[u][:].rearrange("p (i s) -> p s i", i=2)[:, c0 : c0 + GROUP, :])
 
-        def weave_singles(copy, s0, count, u):
-            c0 = s0 - VECTOR_SLOTS
-            slots = grouped[:, s0 * PACK : (s0 + count) * PACK].rearrange("p (s j) -> p s j", j=PACK)
-            copy(slots[:, :, 2 * u : 2 * u + 2], singles[u][:].rearrange("p (i s) -> p s i", i=2)[:, c0 : c0 + count, :])
+        def quantise(g):
+            nc.vector.quantize_mx(out=codes[g][:].bitcast(FP8X4), scales=scales[g][:], in_=grouped[g][:])
 
-        def quantise(s0, count):
-            g, c0 = divmod(s0, GROUP)
-            nc.vector.quantize_mx(
-                out=codes[g][:, c0 : c0 + count].bitcast(FP8X4),
-                scales=scales[g][:, c0 : c0 + count],
-                in_=grouped[:, s0 * PACK : (s0 + count) * PACK],
-            )
-
-        def experts(first, count, h):
-            acc = psum.tile([P, PAIR], F32, name="acc")
-            for k in range(count):
-                e = first + k
-                i, c0 = divmod(e * C, GROUP)
-                col = (e % 2) * N + h * P
+        def experts(g, h):
+            acc = psum.tile([P, GROUP], F32, name="acc")
+            for k in range(2):
+                e = 2 * g + k
+                col = (e % 4) * N + h * P
                 nc.tensor.matmul_mx(
                     out=acc[:, k * C : (k + 1) * C],
-                    lhsT=w_codes[e // 2][:, col * PACK : (col + P) * PACK].bitcast(FP8X4),
-                    lhsT_scale=w_planes[e // PLANES][4 * (e % PLANES) : P, h * P : (h + 1) * P],
-                    rhs=codes[i][:, c0 : c0 + C].bitcast(FP8X4),
-                    rhs_scale=scales[i][:, c0 : c0 + C],
+                    lhsT=w_codes[e // 4][:, col * PACK : (col + P) * PACK].bitcast(FP8X4),
+                    lhsT_scale=w_planes[:, e * N + h * P : e * N + (h + 1) * P],
+                    rhs=codes[g][:, k * C : (k + 1) * C].bitcast(FP8X4),
+                    rhs_scale=scales[g][:, k * C : (k + 1) * C],
                     start=True,
                     stop=True,
                 )
-            for k in range(count):
-                e = first + k
+            for k in range(2):
+                e = 2 * g + k
                 nc.scalar.activation(y[h][:, e * C : (e + 1) * C], acc[:, k * C : (k + 1) * C], GELU, bias=bias[:, h, e : e + 1])
 
-        def scatter(window, s0, count, h):
-            slots = slice(s0, s0 + count)
-            nc.vector.tensor_tensor(window[:].indirect(lists(s0, count)), y[h][:, slots], gates[:, slots], MULT)
+        scalar_cuts = [
+            [GROUP + HELP, S],
+            [GROUP + HELP, 3 * GROUP, S],
+            [GROUP, S],
+            [GROUP, 2 * GROUP, 3 * GROUP, S],
+        ]
+        for j in range(PACK):
+            nc.vector.tensor_copy(slots_of(0)[:, :, j], raw[j][:].indirect(lists(0, GROUP)))
+            cuts = scalar_cuts[j]
+            if cuts[0] > GROUP:
+                nc.vector.tensor_copy(single_row(GROUP, cuts[0], j), raw[j][:].indirect(lists(GROUP, cuts[0])))
+            for s0, s1 in zip(cuts, cuts[1:]):
+                nc.scalar.activation(single_row(s0, s1, j), raw[j][:].indirect(lists(s0, s1)), COPY)
+            if j == 1:
+                for g in range(1, GROUPS):
+                    weave(nc.vector.tensor_copy, g, 0)
+        weave(nc.vector.tensor_copy, 1, 1)
+        quantise(0)
+        quantise(1)
+        weave(nc.vector.tensor_copy, 2, 1)
+        weave(nc.vector.tensor_copy, 3, 1)
+        quantise(2)
+        quantise(3)
+        for g in range(GROUPS):
+            for h in (1, 0):
+                experts(g, h)
 
-        def add_and_store(h, window, queue):
+        cuts = [0, GROUP, GROUP + SCALAR_SCATTER, S]
+
+        def product(s0, s1):
+            nc.vector.tensor_tensor(gated[:, s0:s1], y[1][:, s0:s1], gates[:, s0:s1], MULT)
+
+        def scatter(s0, s1):
+            nc.vector.tensor_tensor(windows[0][:].indirect(lists(s0, s1)), y[0][:, s0:s1], gates[:, s0:s1], MULT)
+
+        product(0, GROUP)
+        scatter(0, GROUP)
+        for s0, s1 in zip(cuts[1:], cuts[2:]):
+            product(s0, s1)
+        scatter(GROUP, S)
+        for s0, s1 in zip(cuts, cuts[1:]):
+            nc.scalar.activation(windows[1][:].indirect(lists(s0, s1)), gated[:, s0:s1], COPY)
+        for h in range(HALVES):
             for t0, width in STORES:
                 cols = slice(t0, t0 + width)
-                nc.vector.tensor_tensor(total[h][:, cols], window[:, cols], residual[h][:, cols], ADD)
-                queue.dma_start(out[h * P : (h + 1) * P, cols], total[h][:, cols])
-
-        for j in range(PACK):
-            last = j == PACK - 1
-            cuts = [0, PIECE, VECTOR_SLOTS] if last else [0, VECTOR_SLOTS]
-            for s0, s1 in zip(cuts, cuts[1:]):
-                nc.vector.tensor_copy(pair_row(s0, s1 - s0, j), raw[j][:].indirect(lists(s0, s1 - s0)))
-            cuts = [VECTOR_SLOTS, S - PIECE, S] if j % 2 else [VECTOR_SLOTS, S]
-            for s0, s1 in zip(cuts, cuts[1:]):
-                nc.scalar.activation(single_row(s0, s1 - s0, j), raw[j][:].indirect(lists(s0, s1 - s0)), COPY)
-            if j == 1:
-                for s0, s1 in zip(cuts, cuts[1:]):
-                    weave_singles(nc.vector.tensor_copy, s0, s1 - s0, 0)
-        weave_pairs(0, PIECE)
-        weave_pairs(PIECE, VECTOR_SLOTS - PIECE)
-        quantise(0, PIECE)
-        weave_singles(nc.vector.tensor_copy, VECTOR_SLOTS, GROUP - VECTOR_SLOTS, 1)
-        weave_singles(nc.vector.tensor_copy, GROUP, PIECE, 1)
-        weave_singles(nc.scalar.copy, S - PIECE, PIECE, 1)
-        for s0 in range(PIECE, S, PIECE):
-            quantise(s0, PIECE)
-        for first, h in [(0, 0), (0, 1), (2, 1), (2, 0), (4, 1), (4, 0), (6, 1), (6, 0)]:
-            experts(first, 2, h)
-        scatter(windows[0], 0, PAIR, 0)
-        gated = [
-            keep.tile([P, FIRST_GATED], F32, name="gated0", tag=f"w_codes{E // 2 - 1}", align_bytes=64),
-            keep.tile([P, S - FIRST_GATED], F32, name="gated1", align_bytes=64),
-        ]
-        nc.vector.tensor_tensor(gated[0][:], y[1][:, 0:FIRST_GATED], gates[:, 0:FIRST_GATED], MULT)
-        nc.vector.tensor_tensor(gated[1][:], y[1][:, FIRST_GATED:S], gates[:, FIRST_GATED:S], MULT)
-        scatter(windows[0], PAIR, S - PAIR, 0)
-        rest = (S - FIRST_GATED) // 2
-        nc.scalar.activation(windows[1][:].indirect(lists(0, FIRST_GATED)), gated[0][:], COPY)
-        for c0 in (0, rest):
-            nc.scalar.activation(windows[1][:].indirect(lists(FIRST_GATED + c0, rest)), gated[1][:, c0 : c0 + rest], COPY)
-        for h in range(HALVES):
-            add_and_store(h, windows[h], (nc.sync, nc.scalar)[h])
+                nc.vector.tensor_tensor(total[h][:, cols], windows[h][:, cols], residual[h][:, cols], ADD)
+                (nc.sync, nc.scalar)[h].dma_start(out[h * P : (h + 1) * P, cols], total[h][:, cols])

@@ -27,7 +27,7 @@ GROUP = 2 * C
 GROUPS = S // GROUP
 PLAIN = S - GROUP
 HELP = 128
-SCALAR_SCATTER = 384
+LAST = 192
 STORES = [(0, 256), (256, 512), (768, 512), (1280, 256)]
 
 
@@ -149,7 +149,7 @@ def tile_moe_res_lin_gelu_kernel(tc, xT, xr, w_words, w_scales, b, gate, offs, o
             for h in (1, 0):
                 experts(g, h)
 
-        cuts = [0, GROUP, GROUP + SCALAR_SCATTER, S]
+        cuts = [0, GROUP, GROUP + 288, S - LAST, S]
 
         def product(s0, s1):
             nc.vector.tensor_tensor(gated[:, s0:s1], y[1][:, s0:s1], gates[:, s0:s1], MULT)
@@ -159,9 +159,9 @@ def tile_moe_res_lin_gelu_kernel(tc, xT, xr, w_words, w_scales, b, gate, offs, o
 
         product(0, GROUP)
         scatter(0, GROUP)
-        for s0, s1 in zip(cuts[1:], cuts[2:]):
-            product(s0, s1)
+        product(GROUP, S - LAST)
         scatter(GROUP, S)
+        product(S - LAST, S)
         for s0, s1 in zip(cuts, cuts[1:]):
             nc.scalar.activation(windows[1][:].indirect(lists(s0, s1)), gated[:, s0:s1], COPY)
         for h in range(HALVES):

@@ -28,7 +28,7 @@ GROUPS = S // GROUP
 PLAIN = S - GROUP
 HELP = 128
 LAST = 192
-STORES = [(0, 256), (256, 512), (768, 512), (1280, 256)]
+STORES = [(256, 256, 512, 512), (512, 512, 256, 256)]
 
 
 def tile_moe_res_lin_gelu_kernel(tc, xT, xr, w_words, w_scales, b, gate, offs, out):
@@ -165,7 +165,8 @@ def tile_moe_res_lin_gelu_kernel(tc, xT, xr, w_words, w_scales, b, gate, offs, o
         for s0, s1 in zip(cuts, cuts[1:]):
             nc.scalar.activation(windows[1][:].indirect(lists(s0, s1)), gated[:, s0:s1], COPY)
         for h in range(HALVES):
-            for t0, width in STORES:
+            for i, width in enumerate(STORES[h]):
+                t0 = sum(STORES[h][:i])
                 cols = slice(t0, t0 + width)
                 nc.vector.tensor_tensor(total[h][:, cols], windows[h][:, cols], residual[h][:, cols], ADD)
                 (nc.sync, nc.scalar)[h].dma_start(out[h * P : (h + 1) * P, cols], total[h][:, cols])

from contextlib import ExitStack

import concourse.mybir as mybir

K, T, E, C, N = 512, 1536, 8, 128, 256
P = 128
PACK = 4
S = E * C
HALVES = N // P

F32 = mybir.dt.float32
BF16 = mybir.dt.bfloat16
I32 = mybir.dt.int32
U32 = mybir.dt.uint32
U16 = mybir.dt.uint16
U8 = mybir.dt.uint8
FP8X4 = mybir.dt.float8_e4m3fn_x4
ADD = mybir.AluOpType.add
MULT = mybir.AluOpType.mult
GELU = mybir.ActivationFunctionType.Gelu_apprx_tanh
COPY = mybir.ActivationFunctionType.Copy

FLOPS = 2 * K * N * S
BYTES = 4 * K * T + 4 * N * T + E * K * N + E * (K // 32) * N + 4 * N * E + 4 * S + 2 * S + 4 * N * T

GROUP = 2 * C
GROUPS = S // GROUP
PLAIN = S - GROUP
HELP = 128
LAST = 192
STORES = [(256, 256, 512, 512), (512, 512, 256, 256)]


def tile_moe_res_lin_gelu_kernel(tc, xT, xr, w_words, w_scales, b, gate, offs, out):
    nc = tc.nc
    with ExitStack() as ctx:
        keep = ctx.enter_context(tc.tile_pool(name="keep", bufs=1))
        psum = ctx.enter_context(tc.psum_pool(name="psum", bufs=8))

        offsets = keep.tile([P, S // 16], U16, name="offsets")
        w_codes = [keep.tile([P, 4 * N * PACK], U8, name=f"w_codes{i}", align_bytes=64) for i in range(2)]
        w_planes = keep.tile([P, E * N], U8, name="w_planes", align_bytes=64)
        bias = keep.tile([P, HALVES, E], F32, name="bias")
        gates = keep.tile([P, S], F32, name="gates")
        raw = [keep.tile([P, T], F32, name=f"raw{j}", align_bytes=64) for j in range(PACK)]
        warm = keep.tile([P, 1], F32, name="warm")
        warm_out = keep.tile([P, 1], F32, name="warm_out")
        windows = [keep.tile([P, T], F32, name=f"window{i}", align_bytes=64) for i in range(2)]
        residual = [keep.tile([P, T], F32, name=f"residual{h}", align_bytes=64) for h in range(HALVES)]
        total = [keep.tile([P, T], F32, name=f"total{h}", align_bytes=64) for h in range(HALVES)]
        y = [keep.tile([P, S], F32, name=f"y{h}", align_bytes=64) for h in range(HALVES)]
        gated = keep.tile([P, S], F32, name="gated", align_bytes=64)
        singles = [keep.tile([P, 2 * PLAIN], BF16, name=f"singles{u}", align_bytes=64) for u in range(2)]
        grouped = [keep.tile([P, GROUP * PACK], BF16, name=f"grouped{g}", align_bytes=64) for g in range(GROUPS)]
        codes = [keep.tile([P, GROUP], U32, name=f"x_codes{g}", align_bytes=64) for g in range(GROUPS)]
        scales = [keep.tile([P, GROUP], U8, name=f"x_scales{g}", align_bytes=64) for g in range(GROUPS)]

        nc.vector.memset(w_planes[:].bitcast(I32), 0)
        nc.vector.memset(warm[:], 0.0)
        nc.scalar.activation(warm_out[:], warm[:], GELU)
        for window in windows:
            nc.vector.memset(window[:].bitcast(I32), 0)

        rows = xT.rearrange("(p j) t -> p j t", j=PACK)

        for j in range(PACK):
            nc.sync.dma_start(raw[j][:], rows[:, j, :])
            if j == 0:
                nc.sync.dma_start(offsets[:], offs)

        def load_weights(i):
            nc.sync.dma_start(
                w_codes[i][:].bitcast(I32).rearrange("p (e n) -> p e n", e=4),
                w_words[4 * i : 4 * i + 4, 0].rearrange("e p n r -> p e (n r)").bitcast(I32),
            )

        load_weights(0)
        for q in range(4):
            nc.sync.dma_start(
                w_planes[32 * q : 32 * q + 4, :].bitcast(I32).rearrange("r (e n) -> r e n", e=E),
                w_scales[:, 0, 4 * q : 4 * q + 4, :].rearrange("e r n -> r e n").bitcast(I32),
            )
        nc.sync.dma_start(bias[:], b.rearrange("(h p) e -> p h e", p=P))
        load_weights(1)
        nc.sync.dma_start(gates[:, 0:GROUP], gate[0:P, 0:GROUP])
        nc.sync.dma_start(gates[:, GROUP:S], gate[0:P, GROUP:S])
        nc.sync.dma_start(residual[0][:], xr[0:P, :])
        nc.sync.dma_start(residual[1][:], xr[P:N, :])

        def lists(s0, s1):
            return offsets[:, s0 // 16 : s1 // 16]

        def slots_of(g):
            return grouped[g][:].rearrange("p (s j) -> p s j", j=PACK)

        def single_row(s0, s1, j):
            first = (j % 2) * PLAIN - GROUP
            return singles[j // 2][:, first + s0 : first + s1]

        def weave(copy, g, u):
            c0 = (g - 1) * GROUP
            copy(slots_of(g)[:, :, 2 * u : 2 * u + 2], singles[u][:].rearrange("p (i s) -> p s i", i=2)[:, c0 : c0 + GROUP, :])

        def quantise(g):
            nc.vector.quantize_mx(out=codes[g][:].bitcast(FP8X4), scales=scales[g][:], in_=grouped[g][:])

        def experts(g, h):
            acc = psum.tile([P, GROUP], F32, name="acc")
            for k in range(2):
                e = 2 * g + k
                col = (e % 4) * N + h * P
                nc.tensor.matmul_mx(
                    out=acc[:, k * C : (k + 1) * C],
                    lhsT=w_codes[e // 4][:, col * PACK : (col + P) * PACK].bitcast(FP8X4),
                    lhsT_scale=w_planes[:, e * N + h * P : e * N + (h + 1) * P],
                    rhs=codes[g][:, k * C : (k + 1) * C].bitcast(FP8X4),
                    rhs_scale=scales[g][:, k * C : (k + 1) * C],
                    start=True,
                    stop=True,
                )
            for k in range(2):
                e = 2 * g + k
                nc.scalar.activation(y[h][:, e * C : (e + 1) * C], acc[:, k * C : (k + 1) * C], GELU, bias=bias[:, h, e : e + 1])

        scalar_cuts = [
            [GROUP + HELP, S],
            [GROUP + HELP, 3 * GROUP, S],
            [GROUP, S],
            [GROUP, 2 * GROUP, 3 * GROUP, S],
        ]
        for j in range(PACK):
            nc.vector.tensor_copy(slots_of(0)[:, :, j], raw[j][:].indirect(lists(0, GROUP)))
            cuts = scalar_cuts[j]
            if cuts[0] > GROUP:
                nc.vector.tensor_copy(single_row(GROUP, cuts[0], j), raw[j][:].indirect(lists(GROUP, cuts[0])))
            for s0, s1 in zip(cuts, cuts[1:]):
                nc.scalar.activation(single_row(s0, s1, j), raw[j][:].indirect(lists(s0, s1)), COPY)
            if j == 1:
                for g in range(1, GROUPS):
                    weave(nc.vector.tensor_copy, g, 0)
        weave(nc.vector.tensor_copy, 1, 1)
        quantise(0)
        quantise(1)
        weave(nc.vector.tensor_copy, 2, 1)
        weave(nc.vector.tensor_copy, 3, 1)
        quantise(2)
        quantise(3)
        for g in range(GROUPS):
            for h in (1, 0):
                experts(g, h)

        cuts = [0, GROUP, GROUP + 288, S - LAST, S]

        def product(s0, s1):
            nc.vector.tensor_tensor(gated[:, s0:s1], y[1][:, s0:s1], gates[:, s0:s1], MULT)

        def scatter(s0, s1):
            nc.vector.tensor_tensor(windows[0][:].indirect(lists(s0, s1)), y[0][:, s0:s1], gates[:, s0:s1], MULT)

        product(0, GROUP)
        scatter(0, GROUP)
        product(GROUP, S - LAST)
        scatter(GROUP, S)
        product(S - LAST, S)
        for s0, s1 in zip(cuts, cuts[1:]):
            nc.scalar.activation(windows[1][:].indirect(lists(s0, s1)), gated[:, s0:s1], COPY)
        for h in range(HALVES):
            for i, width in enumerate(STORES[h]):
                t0 = sum(STORES[h][:i])
                cols = slice(t0, t0 + width)
                nc.vector.tensor_tensor(total[h][:, cols], windows[h][:, cols], residual[h][:, cols], ADD)
                (nc.sync, nc.scalar)[h].dma_start(out[h * P : (h + 1) * P, cols], total[h][:, cols])
